import numpy as np
import ml_dtypes


def mxq(x, axis, fmt="e4m3"):
    dtype, down = {"e4m3": (ml_dtypes.float8_e4m3fn, 7), "e5m2": (ml_dtypes.float8_e5m2, 14)}[fmt]
    v = np.moveaxis(np.asarray(x, np.float32).astype(ml_dtypes.bfloat16).astype(np.float64), axis, -1)
    blocks = v.reshape(v.shape[:-1] + (-1, 32))
    amax = np.abs(blocks).max(-1, keepdims=True)
    byte = np.maximum(np.where(amax > 0, np.frexp(amax)[1] - 1 + 127, 0) - down, 1)
    scale = np.exp2(byte - 127.0)
    codes = (blocks / scale).astype(np.float32).astype(dtype).astype(np.float64)
    return np.moveaxis((codes * scale).reshape(v.shape), -1, axis)


WIDE = False


def mx_kscale(k):
    if not WIDE:
        return np.ones(k)
    levels = np.array([10, -10, 5, -5, 0])
    if k % 512:
        return np.exp2(np.random.permutation(np.resize(levels, k // 32))).repeat(32)
    a = np.empty((k // 512, 16))
    for p in range(k // 512):
        a[p, :8] = np.random.permutation(np.resize(levels, 8))
        for g in range(8):
            far = levels[np.abs(levels - a[p, g]) >= 10]
            a[p, g + 8] = far[np.random.randint(len(far))]
    return np.exp2(a.ravel()).repeat(32)


def f64(x):
    return np.asarray(x).astype(np.float64)


def striped(idx):
    return np.tile(np.asarray(idx).reshape(-1, 16).T, (8, 1)).astype(np.uint16)


def unstriped(offs):
    return offs[:16].T.reshape(-1).astype(np.int64)


E2M1 = np.array([0.0, 0.5, 1.0, 1.5, 2.0, 3.0, 4.0, 6.0, -0.0, -0.5, -1.0, -1.5, -2.0, -3.0, -4.0, -6.0])


def pack_weight(w, fmt):
    k, n = w.shape
    w = f64(np.asarray(w, np.float32).astype(ml_dtypes.bfloat16)).reshape(k // 32, 32, n)
    amax = np.abs(w).max(1)
    if fmt == "e4m3":
        byte = np.frexp(amax)[1] - 1 + 127 - 7
    else:
        mant, ex = np.frexp(amax / 6.0)
        byte = np.where(mant > 0.5, ex, ex - 1) + 127
    byte = np.clip(np.where(amax > 0, byte, 1), 1, 254)
    scaled = (w * np.exp2(127.0 - byte)[:, None, :]).reshape(k, n).astype(np.float32)
    by_word = np.ascontiguousarray(scaled.reshape(k // 512, 128, 4, n).transpose(0, 1, 3, 2))
    if fmt == "e4m3":
        words = by_word.astype(ml_dtypes.float8_e4m3fn).view(np.uint8)
    else:
        c = by_word.astype(ml_dtypes.float4_e2m1fn).view(np.uint8) & 0xF
        words = (c[..., 0::2] | (c[..., 1::2] << 4)).reshape(k // 512, 128, 2 * n)
    return np.ascontiguousarray(words), np.ascontiguousarray(byte.astype(np.uint8).reshape(k // 512, 16, n))


def unpack_weight(words, scales, fmt):
    g, _, n = scales.shape
    words = np.ascontiguousarray(words).reshape(g, 128, n, -1)
    if fmt == "e4m3":
        vals = words.view(ml_dtypes.float8_e4m3fn).astype(np.float64)
    else:
        nib = np.empty((g, 128, n, 4), np.uint8)
        nib[..., 0::2] = words & 0xF
        nib[..., 1::2] = words >> 4
        vals = E2M1[nib]
    vals = vals * np.repeat(np.exp2(scales.astype(np.float64) - 127.0), 8, axis=1)[..., None]
    return vals.transpose(0, 1, 3, 2).reshape(g * 512, n)


B, N, T, D, NQ = 1, 512, 2048, 512, 512


def setup_inputs():
    n = np.random.standard_normal
    idx = np.random.permutation(T)[:B * N]
    s = mx_kscale(D)[:, None]
    kp = pack_weight(n((D, T)) / s, "e4m3")
    return {
        "qT": (n((B, D, NQ)) * s * (1.00 / np.sqrt(D))).astype(np.float32),
        "k_words": kp[0],
        "k_scales": kp[1],
        "nb": np.tile(0.5 * n(2048), (128, 1)).astype(np.float32),
        "offs": striped(idx),
    }


def reference(qT, k_words, k_scales, nb, offs):
    idx = unstriped(offs)
    pick = lambda x, which: x[:, which].reshape(x.shape[0], B, -1).transpose(1, 0, 2)
    k = unpack_weight(k_words, k_scales, "e4m3")
    kg = pick(k, idx)
    qq = mxq(f64(qT), 1, "e4m3")
    a = kg.transpose(0, 2, 1) @ qq
    y = np.maximum(a + pick(f64(nb), idx)[:, :1, :].transpose(0, 2, 1), 0.0)
    return y

@@ -1,0 +1,131 @@
+from contextlib import ExitStack
+
+import concourse.mybir as mybir
+from concourse.masks import make_identity
+
+F32 = mybir.dt.float32
+BF16 = mybir.dt.bfloat16
+I32 = mybir.dt.int32
+U32 = mybir.dt.uint32
+U16 = mybir.dt.uint16
+U8 = mybir.dt.uint8
+FP8X4 = mybir.dt.float8_e4m3fn_x4
+RELU = mybir.ActivationFunctionType.Relu
+ADD = mybir.AluOpType.add
+MAX = mybir.AluOpType.max
+
+P = 128
+PACK = 4
+T = 2048
+SLOTS = 512
+NQ = 512
+HALF = 256
+FLOPS = 2 * 512 * SLOTS * NQ
+BYTES = 4 * 512 * NQ + 512 * T + 16 * T + 4 * T + 2 * P * SLOTS // 16 + 4 * SLOTS * NQ
+
+
+def tile_attend_neut_relu_topk_kernel(tc, qT, k_words, k_scales, nb, offs, out):
+    nc = tc.nc
+    with ExitStack() as ctx:
+        keep = ctx.enter_context(tc.tile_pool(name="keep", bufs=1))
+        psum = ctx.enter_context(tc.psum_pool(name="psum", bufs=1))
+
+        offsets = keep.tile([P, SLOTS // 16], U16, name="offsets")
+        nc.sync.dma_start(offsets[:], offs)
+
+        scale_table = keep.tile([P, T], U8, name="scale_table", align_bytes=64)
+        nc.vector.memset(scale_table[:].bitcast(I32), 0)
+        bias_table = keep.tile([P, T], F32, name="bias_table")
+        nc.vector.memset(bias_table[:], 0.0)
+
+        q_rows = qT[0].rearrange("(p t) q -> p t q", t=PACK)
+        q_raw = [keep.tile([P, PACK, HALF], F32, name="q_raw%d" % h) for h in range(2)]
+        nc.sync.dma_start(q_raw[0][:], q_rows[:, :, 0:HALF])
+        word_table = keep.tile([P, T], I32, name="word_table")
+        nc.sync.dma_start(word_table[:], k_words[0].rearrange("p n r -> p (n r)").bitcast(I32))
+        nc.sync.dma_start(q_raw[1][:], q_rows[:, :, HALF:NQ])
+
+        scale_rows = k_scales[0].bitcast(I32)
+        for r in range(4):
+            nc.scalar.dma_start(scale_table[r:P:32, :].bitcast(I32), scale_rows[r:16:4, :])
+        nc.scalar.dma_start(bias_table[16:17, :], nb[16:17, :])
+
+        identity = keep.tile([P, P], F32, name="identity")
+        make_identity(nc, identity[:])
+        warm = keep.tile([P, 1], F32, name="warm")
+        nc.scalar.activation(warm[:], identity[:, 0:1], RELU)
+
+        def interleave(engine, h, c0, c1, grouped):
+            src = q_raw[h][:, :, c0:c1].rearrange("p t (c i) -> p c t i", i=4)
+            dst = grouped[:, c0:c1, :].rearrange("p (c i) t -> p c t i", i=4)
+            if engine == "scalar":
+                nc.scalar.copy(dst, src)
+            else:
+                nc.vector.tensor_copy(dst, src)
+
+        grouped = [keep.tile([P, HALF, PACK], BF16, name="grouped%d" % h, align_bytes=64) for h in range(2)]
+        q_codes = [keep.tile([P, HALF], U32, name="q_codes%d" % h, align_bytes=64) for h in range(2)]
+        q_scales = [keep.tile([P, HALF], U8, name="q_scales%d" % h, align_bytes=64) for h in range(2)]
+
+        def quantise(h, c0, c1):
+            nc.vector.quantize_mx(
+                out=q_codes[h][:, c0:c1].bitcast(FP8X4),
+                scales=q_scales[h][:, c0:c1],
+                in_=grouped[h][:, c0:c1, :].rearrange("p c t -> p (c t)"),
+            )
+
+        interleave("scalar", 0, 0, HALF, grouped[0])
+
+        k_scale = keep.tile([P, SLOTS], U8, name="k_scale", align_bytes=64)
+        nc.vector.tensor_copy(k_scale[:], scale_table[:].indirect(offsets[:]))
+        bias_row = keep.tile([P, SLOTS], F32, name="bias_row")
+        nc.vector.tensor_copy(bias_row[:], bias_table[:].indirect(offsets[:]))
+        turned = psum.tile([P, 4, P], F32, name="turned", tag="bank7")
+        for j in range(4):
+            nc.tensor.transpose(turned[:, j, :], bias_row[:, j * P : (j + 1) * P], identity[:])
+        bias = keep.tile([P, 4], F32, name="bias")
+        nc.scalar.copy(bias[:], turned[:, :, 16])
+
+        quantise(0, 0, HALF)
+
+        k_codes = [keep.tile([P, HALF], U32, name="k_codes%d" % g, align_bytes=64) for g in range(2)]
+        for g in range(2):
+            nc.vector.tensor_copy(k_codes[g][:], word_table[:].bitcast(U32).indirect(offsets[:, 16 * g : 16 * (g + 1)]))
+
+        out_rows = out[0].rearrange("(j p) q -> p j q", p=P)
+
+        def product(acc, j, h, c0, c1):
+            nc.tensor.matmul_mx(
+                out=acc,
+                lhsT=k_codes[j // 2][:, (j % 2) * P : (j % 2 + 1) * P].bitcast(FP8X4),
+                lhsT_scale=k_scale[:, j * P : (j + 1) * P],
+                rhs=q_codes[h][:, c0:c1].bitcast(FP8X4),
+                rhs_scale=q_scales[h][:, c0:c1],
+                start=True,
+                stop=True,
+            )
+
+        def finish(engine, dst, acc, j):
+            if engine == "scalar":
+                nc.scalar.activation(dst, acc, RELU, bias=bias[:, j : j + 1])
+            else:
+                nc.vector.tensor_scalar(dst, acc, bias[:, j : j + 1], 0.0, ADD, MAX)
+
+        result = [keep.tile([P, 4, HALF], F32, name="result%d" % h) for h in range(2)]
+        for j in range(4):
+            acc = psum.tile([P, HALF], F32, name="acc_a%d" % j, tag="bank%d" % j)
+            product(acc[:], j, 0, 0, HALF)
+            finish("scalar", result[0][:, j, :], acc[:], j)
+            if j % 2 == 1:
+                nc.sync.dma_start(out_rows[:, j - 1 : j + 1, 0:HALF], result[0][:, j - 1 : j + 1, :])
+
+        interleave("vector", 1, 0, P, grouped[1])
+        interleave("scalar", 1, P, HALF, grouped[1])
+        quantise(1, 0, P)
+        quantise(1, P, HALF)
+        for j in range(4):
+            acc = psum.tile([P, HALF], F32, name="acc_b%d" % j, tag="bank%d" % (4 + j))
+            product(acc[:], j, 1, 0, HALF)
+            finish("vector" if j % 2 == 1 else "scalar", result[1][:, j, :], acc[:], j)
+            if j % 2 == 1:
+                nc.sync.dma_start(out_rows[:, j - 1 : j + 1, HALF:NQ], result[1][:, j - 1 : j + 1, :])

@@ -10,18 +10,28 @@ U32 = mybir.dt.uint32
 U16 = mybir.dt.uint16
 U8 = mybir.dt.uint8
 FP8X4 = mybir.dt.float8_e4m3fn_x4
+COPY = mybir.ActivationFunctionType.Copy
 RELU = mybir.ActivationFunctionType.Relu
 ADD = mybir.AluOpType.add
 MAX = mybir.AluOpType.max
 
 P = 128
 PACK = 4
-T = 2048
-SLOTS = 512
-NQ = 512
-HALF = 256
-FLOPS = 2 * 512 * SLOTS * NQ
-BYTES = 4 * 512 * NQ + 512 * T + 16 * T + 4 * T + 2 * P * SLOTS // 16 + 4 * SLOTS * NQ
+FEATURES = P * PACK
+NEURONS = 2048
+LISTED = 512
+QUERIES = 512
+TILES = LISTED // P
+HALF = QUERIES // 2
+QUARTER = HALF // 2
+BLOCKS = FEATURES // 32
+QUADRANT = 32
+BANKS = 8
+LINE = 4
+BIAS_ROW = 16
+
+FLOPS = 2 * FEATURES * LISTED * QUERIES
+BYTES = 4 * FEATURES * QUERIES + (FEATURES + BLOCKS + 4) * NEURONS + 2 * P * LISTED // 16 + 4 * LISTED * QUERIES
 
 
 def tile_attend_neut_relu_topk_kernel(tc, qT, k_words, k_scales, nb, offs, out):
@@ -30,102 +40,111 @@ def tile_attend_neut_relu_topk_kernel(tc, qT, k_words, k_scales, nb, offs, out):
         keep = ctx.enter_context(tc.tile_pool(name="keep", bufs=1))
         psum = ctx.enter_context(tc.psum_pool(name="psum", bufs=1))
 
-        offsets = keep.tile([P, SLOTS // 16], U16, name="offsets")
+        offsets = keep.tile([P, LISTED // 16], U16, name="offsets")
         nc.sync.dma_start(offsets[:], offs)
 
-        scale_table = keep.tile([P, T], U8, name="scale_table", align_bytes=64)
+        scale_table = keep.tile([P, NEURONS], U8, name="scale_table", align_bytes=64)
         nc.vector.memset(scale_table[:].bitcast(I32), 0)
-        bias_table = keep.tile([P, T], F32, name="bias_table")
-        nc.vector.memset(bias_table[:], 0.0)
+        bias_table = keep.tile([P, NEURONS], F32, name="bias_table", tag="bias_then_codes", align_bytes=64)
+        nc.vector.memset(bias_table[:].bitcast(I32), 0)
+        word_table = keep.tile([P, NEURONS], I32, name="word_table")
 
-        q_rows = qT[0].rearrange("(p t) q -> p t q", t=PACK)
-        q_raw = [keep.tile([P, PACK, HALF], F32, name="q_raw%d" % h) for h in range(2)]
-        nc.sync.dma_start(q_raw[0][:], q_rows[:, :, 0:HALF])
-        word_table = keep.tile([P, T], I32, name="word_table")
-        nc.sync.dma_start(word_table[:], k_words[0].rearrange("p n r -> p (n r)").bitcast(I32))
-        nc.sync.dma_start(q_raw[1][:], q_rows[:, :, HALF:NQ])
-
+        q_planes = qT[0].rearrange("(p t) q -> p t q", t=PACK)
         scale_rows = k_scales[0].bitcast(I32)
+        q_raw = [keep.tile([P, PACK, HALF], F32, name="q_raw%d" % h) for h in range(2)]
+        nc.sync.dma_start(q_raw[0][:, 0:2, :], q_planes[:, 0:2, 0:HALF])
         for r in range(4):
-            nc.scalar.dma_start(scale_table[r:P:32, :].bitcast(I32), scale_rows[r:16:4, :])
-        nc.scalar.dma_start(bias_table[16:17, :], nb[16:17, :])
+            nc.sync.dma_start(scale_table[r:P:QUADRANT, :].bitcast(I32), scale_rows[r:BLOCKS:4, :])
+        nc.sync.dma_start(q_raw[0][:, 2:4, :], q_planes[:, 2:4, 0:HALF])
+        nc.sync.dma_start(bias_table[BIAS_ROW : BIAS_ROW + 1, :], nb[BIAS_ROW : BIAS_ROW + 1, :])
+        nc.sync.dma_start(word_table[:], k_words[0].rearrange("p n r -> p (n r)").bitcast(I32))
+        nc.sync.dma_start(q_raw[1][:], q_planes[:, :, HALF:QUERIES])
 
         identity = keep.tile([P, P], F32, name="identity")
-        make_identity(nc, identity[:])
-        warm = keep.tile([P, 1], F32, name="warm")
-        nc.scalar.activation(warm[:], identity[:, 0:1], RELU)
+        nc.vector.memset(identity[:], 0.0)
+        make_identity(nc, identity[:], nomemset=True)
 
-        def interleave(engine, h, c0, c1, grouped):
-            src = q_raw[h][:, :, c0:c1].rearrange("p t (c i) -> p c t i", i=4)
-            dst = grouped[:, c0:c1, :].rearrange("p (c i) t -> p c t i", i=4)
-            if engine == "scalar":
-                nc.scalar.copy(dst, src)
-            else:
-                nc.vector.tensor_copy(dst, src)
+        grouped, q_scales, result = [], [], []
+        for h in range(2):
+            grouped.append(keep.tile([P, HALF, PACK], BF16, name="grouped%d" % h, align_bytes=64))
+            q_scales.append(keep.tile([P, HALF], U8, name="q_scales%d" % h, align_bytes=64))
+            result.append(keep.tile([P, TILES, HALF], F32, name="result%d" % h))
 
-        grouped = [keep.tile([P, HALF, PACK], BF16, name="grouped%d" % h, align_bytes=64) for h in range(2)]
-        q_codes = [keep.tile([P, HALF], U32, name="q_codes%d" % h, align_bytes=64) for h in range(2)]
-        q_scales = [keep.tile([P, HALF], U8, name="q_scales%d" % h, align_bytes=64) for h in range(2)]
+        def interleave_views(h, rows, planes):
+            dst = grouped[h][:, rows, planes].rearrange("p (c i) t -> p c t i", i=LINE)
+            src = q_raw[h][:, planes, rows].rearrange("p t (c i) -> p c t i", i=LINE)
+            return dst, src
 
-        def quantise(h, c0, c1):
+        def quantise(h, codes, rows):
             nc.vector.quantize_mx(
-                out=q_codes[h][:, c0:c1].bitcast(FP8X4),
-                scales=q_scales[h][:, c0:c1],
-                in_=grouped[h][:, c0:c1, :].rearrange("p c t -> p (c t)"),
+                out=codes[:, rows].bitcast(FP8X4),
+                scales=q_scales[h][:, rows],
+                in_=grouped[h][:, rows, :].rearrange("p c t -> p (c t)"),
             )
 
-        interleave("scalar", 0, 0, HALF, grouped[0])
+        for t0 in (0, 2):
+            nc.scalar.activation(*interleave_views(0, slice(0, HALF), slice(t0, t0 + 2)), COPY)
 
-        k_scale = keep.tile([P, SLOTS], U8, name="k_scale", align_bytes=64)
+        k_scale = keep.tile([P, LISTED], U8, name="k_scale", align_bytes=64)
         nc.vector.tensor_copy(k_scale[:], scale_table[:].indirect(offsets[:]))
-        bias_row = keep.tile([P, SLOTS], F32, name="bias_row")
-        nc.vector.tensor_copy(bias_row[:], bias_table[:].indirect(offsets[:]))
-        turned = psum.tile([P, 4, P], F32, name="turned", tag="bank7")
-        for j in range(4):
-            nc.tensor.transpose(turned[:, j, :], bias_row[:, j * P : (j + 1) * P], identity[:])
-        bias = keep.tile([P, 4], F32, name="bias")
-        nc.scalar.copy(bias[:], turned[:, :, 16])
 
-        quantise(0, 0, HALF)
+        bias_listed = keep.tile([P, LISTED], F32, name="bias_listed")
+        nc.vector.tensor_copy(bias_listed[:], bias_table[:].indirect(offsets[:]))
+        turned = psum.tile([P, TILES, P], F32, name="turned", tag="bank%d" % (BANKS - 1))
+        for j in range(TILES):
+            nc.tensor.transpose(turned[:, j, :], bias_listed[:, j * P : (j + 1) * P], identity[:])
+        bias = keep.tile([P, TILES], F32, name="bias")
+        nc.scalar.copy(bias[:], turned[:, :, BIAS_ROW])
 
-        k_codes = [keep.tile([P, HALF], U32, name="k_codes%d" % g, align_bytes=64) for g in range(2)]
+        q_codes = [keep.tile([P, HALF], U32, name="q_codes0", tag="bias_then_codes", align_bytes=64)]
+        quantise(0, q_codes[0], slice(0, HALF))
+
+        k_codes = []
         for g in range(2):
+            k_codes.append(keep.tile([P, 2 * P], U32, name="k_codes%d" % g, align_bytes=64))
             nc.vector.tensor_copy(k_codes[g][:], word_table[:].bitcast(U32).indirect(offsets[:, 16 * g : 16 * (g + 1)]))
 
-        out_rows = out[0].rearrange("(j p) q -> p j q", p=P)
+        quarters = [slice(0, QUARTER), slice(QUARTER, HALF)]
+        for rows in quarters:
+            nc.vector.tensor_copy(*interleave_views(1, rows, slice(0, PACK)))
+        q_codes.append(keep.tile([P, HALF], U32, name="q_codes1", align_bytes=64))
+        for rows in quarters:
+            quantise(1, q_codes[1], rows)
 
-        def product(acc, j, h, c0, c1):
+        out_tiles = out[0].rearrange("(j p) q -> p j q", p=P)
+
+        def product(bank, j, h, rows):
+            acc = psum.tile([P, rows.stop - rows.start], F32, name="acc", tag="bank%d" % bank)
             nc.tensor.matmul_mx(
-                out=acc,
+                out=acc[:],
                 lhsT=k_codes[j // 2][:, (j % 2) * P : (j % 2 + 1) * P].bitcast(FP8X4),
                 lhsT_scale=k_scale[:, j * P : (j + 1) * P],
-                rhs=q_codes[h][:, c0:c1].bitcast(FP8X4),
-                rhs_scale=q_scales[h][:, c0:c1],
+                rhs=q_codes[h][:, rows].bitcast(FP8X4),
+                rhs_scale=q_scales[h][:, rows],
                 start=True,
                 stop=True,
             )
+            return acc
 
-        def finish(engine, dst, acc, j):
-            if engine == "scalar":
-                nc.scalar.activation(dst, acc, RELU, bias=bias[:, j : j + 1])
+        def finish(on_scalar, acc, j, h, rows):
+            if on_scalar:
+                nc.scalar.activation(result[h][:, j, rows], acc[:], RELU, bias=bias[:, j : j + 1])
             else:
-                nc.vector.tensor_scalar(dst, acc, bias[:, j : j + 1], 0.0, ADD, MAX)
+                nc.vector.tensor_scalar(result[h][:, j, rows], acc[:], bias[:, j : j + 1], 0.0, ADD, MAX)
 
-        result = [keep.tile([P, 4, HALF], F32, name="result%d" % h) for h in range(2)]
-        for j in range(4):
-            acc = psum.tile([P, HALF], F32, name="acc_a%d" % j, tag="bank%d" % j)
-            product(acc[:], j, 0, 0, HALF)
-            finish("scalar", result[0][:, j, :], acc[:], j)
-            if j % 2 == 1:
-                nc.sync.dma_start(out_rows[:, j - 1 : j + 1, 0:HALF], result[0][:, j - 1 : j + 1, :])
+        def store(j, h):
+            nc.sync.dma_start(out_tiles[:, j : j + 1, h * HALF : (h + 1) * HALF], result[h][:, j : j + 1, :])
 
-        interleave("vector", 1, 0, P, grouped[1])
-        interleave("scalar", 1, P, HALF, grouped[1])
-        quantise(1, 0, P)
-        quantise(1, P, HALF)
-        for j in range(4):
-            acc = psum.tile([P, HALF], F32, name="acc_b%d" % j, tag="bank%d" % (4 + j))
-            product(acc[:], j, 1, 0, HALF)
-            finish("vector" if j % 2 == 1 else "scalar", result[1][:, j, :], acc[:], j)
-            if j % 2 == 1:
-                nc.sync.dma_start(out_rows[:, j - 1 : j + 1, HALF:NQ], result[1][:, j - 1 : j + 1, :])
+        for j in range(TILES):
+            acc = product(j, j, 0, slice(0, HALF))
+            finish(True, acc, j, 0, slice(0, HALF))
+            store(j, 0)
+
+        pieces = []
+        for j in range(TILES):
+            for rows in quarters if j in (0, TILES - 1) else [slice(0, HALF)]:
+                pieces.append((j, rows, product((TILES + len(pieces)) % BANKS, j, 1, rows)))
+        for n, (j, rows, acc) in enumerate(pieces):
+            finish(n % 2 == 0, acc, j, 1, rows)
+            if rows.stop == HALF:
+                store(j, 1)

@@ -28,7 +28,7 @@ BLOCKS = FEATURES // 32
 QUADRANT = 32
 BANKS = 8
 LINE = 4
-BIAS_ROW = 16
+BIAS_ROW = P - 1
 
 FLOPS = 2 * FEATURES * LISTED * QUERIES
 BYTES = 4 * FEATURES * QUERIES + (FEATURES + BLOCKS + 4) * NEURONS + 2 * P * LISTED // 16 + 4 * LISTED * QUERIES
@@ -41,28 +41,27 @@ def tile_attend_neut_relu_topk_kernel(tc, qT, k_words, k_scales, nb, offs, out):
         psum = ctx.enter_context(tc.psum_pool(name="psum", bufs=1))
 
         offsets = keep.tile([P, LISTED // 16], U16, name="offsets")
-        nc.sync.dma_start(offsets[:], offs)
 
-        scale_table = keep.tile([P, NEURONS], U8, name="scale_table", align_bytes=64)
+        scale_table = keep.tile([P, NEURONS], U8, name="scale_table", tag="scales_then_codes", align_bytes=64)
         nc.vector.memset(scale_table[:].bitcast(I32), 0)
-        bias_table = keep.tile([P, NEURONS], F32, name="bias_table", tag="bias_then_codes", align_bytes=64)
-        nc.vector.memset(bias_table[:].bitcast(I32), 0)
+        identity = keep.tile([P, P], F32, name="identity")
+        nc.vector.memset(identity[:], 0.0)
+        make_identity(nc, identity[:], nomemset=True)
+        bias_table = keep.tile([P, NEURONS], F32, name="bias_table")
+        nc.vector.memset(bias_table[0:BIAS_ROW, :].bitcast(I32), 0)
         word_table = keep.tile([P, NEURONS], I32, name="word_table")
 
         q_planes = qT[0].rearrange("(p t) q -> p t q", t=PACK)
         scale_rows = k_scales[0].bitcast(I32)
         q_raw = [keep.tile([P, PACK, HALF], F32, name="q_raw%d" % h) for h in range(2)]
         nc.sync.dma_start(q_raw[0][:, 0:2, :], q_planes[:, 0:2, 0:HALF])
+        nc.sync.dma_start(offsets[:], offs)
+        nc.sync.dma_start(bias_table[BIAS_ROW : BIAS_ROW + 1, :], nb[BIAS_ROW : BIAS_ROW + 1, :])
         for r in range(4):
             nc.sync.dma_start(scale_table[r:P:QUADRANT, :].bitcast(I32), scale_rows[r:BLOCKS:4, :])
         nc.sync.dma_start(q_raw[0][:, 2:4, :], q_planes[:, 2:4, 0:HALF])
-        nc.sync.dma_start(bias_table[BIAS_ROW : BIAS_ROW + 1, :], nb[BIAS_ROW : BIAS_ROW + 1, :])
         nc.sync.dma_start(word_table[:], k_words[0].rearrange("p n r -> p (n r)").bitcast(I32))
         nc.sync.dma_start(q_raw[1][:], q_planes[:, :, HALF:QUERIES])
-
-        identity = keep.tile([P, P], F32, name="identity")
-        nc.vector.memset(identity[:], 0.0)
-        make_identity(nc, identity[:], nomemset=True)
 
         grouped, q_scales, result = [], [], []
         for h in range(2):
@@ -85,9 +84,6 @@ def tile_attend_neut_relu_topk_kernel(tc, qT, k_words, k_scales, nb, offs, out):
         for t0 in (0, 2):
             nc.scalar.activation(*interleave_views(0, slice(0, HALF), slice(t0, t0 + 2)), COPY)
 
-        k_scale = keep.tile([P, LISTED], U8, name="k_scale", align_bytes=64)
-        nc.vector.tensor_copy(k_scale[:], scale_table[:].indirect(offsets[:]))
-
         bias_listed = keep.tile([P, LISTED], F32, name="bias_listed")
         nc.vector.tensor_copy(bias_listed[:], bias_table[:].indirect(offsets[:]))
         turned = psum.tile([P, TILES, P], F32, name="turned", tag="bank%d" % (BANKS - 1))
@@ -96,7 +92,10 @@ def tile_attend_neut_relu_topk_kernel(tc, qT, k_words, k_scales, nb, offs, out):
         bias = keep.tile([P, TILES], F32, name="bias")
         nc.scalar.copy(bias[:], turned[:, :, BIAS_ROW])
 
-        q_codes = [keep.tile([P, HALF], U32, name="q_codes0", tag="bias_then_codes", align_bytes=64)]
+        k_scale = keep.tile([P, LISTED], U8, name="k_scale", align_bytes=64)
+        nc.vector.tensor_copy(k_scale[:], scale_table[:].indirect(offsets[:]))
+
+        q_codes = [keep.tile([P, HALF], U32, name="q_codes0", tag="scales_then_codes", align_bytes=64)]
         quantise(0, q_codes[0], slice(0, HALF))
 
         k_codes = []

@@ -22,13 +22,14 @@ NEURONS = 2048
 LISTED = 512
 QUERIES = 512
 TILES = LISTED // P
-HALF = QUERIES // 2
-QUARTER = HALF // 2
 BLOCKS = FEATURES // 32
 QUADRANT = 32
 BANKS = 8
 LINE = 4
 BIAS_ROW = P - 1
+WIDTHS = (256, 128, 128)
+READERS = ("SSSS", "VSVS", "VSVS")
+STORES = ((1, 1, 1, 1,), (2, 2,), (2, 2,))
 
 FLOPS = 2 * FEATURES * LISTED * QUERIES
 BYTES = 4 * FEATURES * QUERIES + (FEATURES + BLOCKS + 4) * NEURONS + 2 * P * LISTED // 16 + 4 * LISTED * QUERIES
@@ -41,7 +42,6 @@ def tile_attend_neut_relu_topk_kernel(tc, qT, k_words, k_scales, nb, offs, out):
         psum = ctx.enter_context(tc.psum_pool(name="psum", bufs=1))
 
         offsets = keep.tile([P, LISTED // 16], U16, name="offsets")
-
         scale_table = keep.tile([P, NEURONS], U8, name="scale_table", tag="scales_then_codes", align_bytes=64)
         nc.vector.memset(scale_table[:].bitcast(I32), 0)
         identity = keep.tile([P, P], F32, name="identity")
@@ -49,40 +49,59 @@ def tile_attend_neut_relu_topk_kernel(tc, qT, k_words, k_scales, nb, offs, out):
         make_identity(nc, identity[:], nomemset=True)
         bias_table = keep.tile([P, NEURONS], F32, name="bias_table")
         nc.vector.memset(bias_table[0:BIAS_ROW, :].bitcast(I32), 0)
-        word_table = keep.tile([P, NEURONS], I32, name="word_table")
+        word_table = keep.tile([P, NEURONS], I32, name="word_table", align_bytes=64)
 
+        chunks = range(len(WIDTHS))
+        starts = [sum(WIDTHS[:c]) for c in chunks]
         q_planes = qT[0].rearrange("(p t) q -> p t q", t=PACK)
         scale_rows = k_scales[0].bitcast(I32)
-        q_raw = [keep.tile([P, PACK, HALF], F32, name="q_raw%d" % h) for h in range(2)]
-        nc.sync.dma_start(q_raw[0][:, 0:2, :], q_planes[:, 0:2, 0:HALF])
+        q_raw = [keep.tile([P, PACK, WIDTHS[c]], F32, name="q_raw%d" % c) for c in chunks]
+
+        def load_queries(c, planes):
+            nc.sync.dma_start(q_raw[c][:, planes, :], q_planes[:, planes, starts[c] : starts[c] + WIDTHS[c]])
+
+        def load_bias_row():
+            nc.sync.dma_start(bias_table[BIAS_ROW : BIAS_ROW + 1, :], nb[BIAS_ROW : BIAS_ROW + 1, :])
+
+        def load_words():
+            nc.sync.dma_start(word_table[:], k_words[0].rearrange("p n r -> p (n r)").bitcast(I32))
+
+        first_parts = [slice(0, PACK)]
         nc.sync.dma_start(offsets[:], offs)
-        nc.sync.dma_start(bias_table[BIAS_ROW : BIAS_ROW + 1, :], nb[BIAS_ROW : BIAS_ROW + 1, :])
+        load_bias_row()
+        load_queries(0, first_parts[0])
         for r in range(4):
             nc.sync.dma_start(scale_table[r:P:QUADRANT, :].bitcast(I32), scale_rows[r:BLOCKS:4, :])
-        nc.sync.dma_start(q_raw[0][:, 2:4, :], q_planes[:, 2:4, 0:HALF])
-        nc.sync.dma_start(word_table[:], k_words[0].rearrange("p n r -> p (n r)").bitcast(I32))
-        nc.sync.dma_start(q_raw[1][:], q_planes[:, :, HALF:QUERIES])
+        for planes in first_parts[1:]:
+            load_queries(0, planes)
+        load_words()
+        for c in chunks[1:]:
+            load_queries(c, slice(0, PACK))
 
-        grouped, q_scales, result = [], [], []
-        for h in range(2):
-            grouped.append(keep.tile([P, HALF, PACK], BF16, name="grouped%d" % h, align_bytes=64))
-            q_scales.append(keep.tile([P, HALF], U8, name="q_scales%d" % h, align_bytes=64))
-            result.append(keep.tile([P, TILES, HALF], F32, name="result%d" % h))
+        grouped, q_scales, q_codes, result = [], [], [None for c in chunks], []
+        for c in chunks:
+            grouped.append(keep.tile([P, WIDTHS[c], PACK], BF16, name="grouped%d" % c, align_bytes=64))
+            q_scales.append(keep.tile([P, WIDTHS[c]], U8, name="q_scales%d" % c, align_bytes=64))
+            result.append(keep.tile([P, TILES, WIDTHS[c]], F32, name="result%d" % c))
 
-        def interleave_views(h, rows, planes):
-            dst = grouped[h][:, rows, planes].rearrange("p (c i) t -> p c t i", i=LINE)
-            src = q_raw[h][:, planes, rows].rearrange("p t (c i) -> p c t i", i=LINE)
-            return dst, src
+        def interleave(engine, c, rows, planes):
+            dst = grouped[c][:, rows, planes].rearrange("p (c i) t -> p c t i", i=LINE)
+            src = q_raw[c][:, planes, rows].rearrange("p t (c i) -> p c t i", i=LINE)
+            if engine == "S":
+                nc.scalar.activation(dst, src, COPY)
+            else:
+                nc.vector.tensor_copy(dst, src)
 
-        def quantise(h, codes, rows):
+        def quantise(c, tag):
+            q_codes[c] = keep.tile([P, WIDTHS[c]], U32, name="q_codes%d" % c, tag=tag, align_bytes=64)
             nc.vector.quantize_mx(
-                out=codes[:, rows].bitcast(FP8X4),
-                scales=q_scales[h][:, rows],
-                in_=grouped[h][:, rows, :].rearrange("p c t -> p (c t)"),
+                out=q_codes[c][:].bitcast(FP8X4),
+                scales=q_scales[c][:],
+                in_=grouped[c][:].rearrange("p c t -> p (c t)"),
             )
 
-        for t0 in (0, 2):
-            nc.scalar.activation(*interleave_views(0, slice(0, HALF), slice(t0, t0 + 2)), COPY)
+        for planes in first_parts:
+            interleave("S", 0, slice(0, WIDTHS[0]), planes)
 
         bias_listed = keep.tile([P, LISTED], F32, name="bias_listed")
         nc.vector.tensor_copy(bias_listed[:], bias_table[:].indirect(offsets[:]))
@@ -95,55 +114,39 @@ def tile_attend_neut_relu_topk_kernel(tc, qT, k_words, k_scales, nb, offs, out):
         k_scale = keep.tile([P, LISTED], U8, name="k_scale", align_bytes=64)
         nc.vector.tensor_copy(k_scale[:], scale_table[:].indirect(offsets[:]))
 
-        q_codes = [keep.tile([P, HALF], U32, name="q_codes0", tag="scales_then_codes", align_bytes=64)]
-        quantise(0, q_codes[0], slice(0, HALF))
+        quantise(0, "scales_then_codes")
 
         k_codes = []
         for g in range(2):
             k_codes.append(keep.tile([P, 2 * P], U32, name="k_codes%d" % g, align_bytes=64))
             nc.vector.tensor_copy(k_codes[g][:], word_table[:].bitcast(U32).indirect(offsets[:, 16 * g : 16 * (g + 1)]))
 
-        quarters = [slice(0, QUARTER), slice(QUARTER, HALF)]
-        for rows in quarters:
-            nc.vector.tensor_copy(*interleave_views(1, rows, slice(0, PACK)))
-        q_codes.append(keep.tile([P, HALF], U32, name="q_codes1", align_bytes=64))
-        for rows in quarters:
-            quantise(1, q_codes[1], rows)
+        interleave("S", 1, slice(0, 128), slice(0, PACK))
+        interleave("V", 2, slice(0, 128), slice(0, PACK))
+        quantise(1, "codes1")
+        quantise(2, "codes2")
 
         out_tiles = out[0].rearrange("(j p) q -> p j q", p=P)
-
-        def product(bank, j, h, rows):
-            acc = psum.tile([P, rows.stop - rows.start], F32, name="acc", tag="bank%d" % bank)
-            nc.tensor.matmul_mx(
-                out=acc[:],
-                lhsT=k_codes[j // 2][:, (j % 2) * P : (j % 2 + 1) * P].bitcast(FP8X4),
-                lhsT_scale=k_scale[:, j * P : (j + 1) * P],
-                rhs=q_codes[h][:, rows].bitcast(FP8X4),
-                rhs_scale=q_scales[h][:, rows],
-                start=True,
-                stop=True,
-            )
-            return acc
-
-        def finish(on_scalar, acc, j, h, rows):
-            if on_scalar:
-                nc.scalar.activation(result[h][:, j, rows], acc[:], RELU, bias=bias[:, j : j + 1])
-            else:
-                nc.vector.tensor_scalar(result[h][:, j, rows], acc[:], bias[:, j : j + 1], 0.0, ADD, MAX)
-
-        def store(j, h):
-            nc.sync.dma_start(out_tiles[:, j : j + 1, h * HALF : (h + 1) * HALF], result[h][:, j : j + 1, :])
-
-        for j in range(TILES):
-            acc = product(j, j, 0, slice(0, HALF))
-            finish(True, acc, j, 0, slice(0, HALF))
-            store(j, 0)
-
-        pieces = []
-        for j in range(TILES):
-            for rows in quarters if j in (0, TILES - 1) else [slice(0, HALF)]:
-                pieces.append((j, rows, product((TILES + len(pieces)) % BANKS, j, 1, rows)))
-        for n, (j, rows, acc) in enumerate(pieces):
-            finish(n % 2 == 0, acc, j, 1, rows)
-            if rows.stop == HALF:
-                store(j, 1)
+        for c in chunks:
+            stored = 0
+            ends = [sum(STORES[c][: n + 1]) for n in range(len(STORES[c]))]
+            for j in range(TILES):
+                acc = psum.tile([P, WIDTHS[c]], F32, name="acc", tag="bank%d" % ((TILES * c + j) % BANKS))
+                nc.tensor.matmul_mx(
+                    out=acc[:],
+                    lhsT=k_codes[j // 2][:, (j % 2) * P : (j % 2 + 1) * P].bitcast(FP8X4),
+                    lhsT_scale=k_scale[:, j * P : (j + 1) * P],
+                    rhs=q_codes[c][:].bitcast(FP8X4),
+                    rhs_scale=q_scales[c][:],
+                    start=True,
+                    stop=True,
+                )
+                if READERS[c][j] == "S":
+                    nc.scalar.activation(result[c][:, j, :], acc[:], RELU, bias=bias[:, j : j + 1])
+                else:
+                    nc.vector.tensor_scalar(result[c][:, j, :], acc[:], bias[:, j : j + 1], 0.0, ADD, MAX)
+                if j + 1 in ends:
+                    nc.sync.dma_start(
+                        out_tiles[:, stored : j + 1, starts[c] : starts[c] + WIDTHS[c]], result[c][:, stored : j + 1, :]
+                    )
+                    stored = j + 1

@@ -27,9 +27,9 @@ QUADRANT = 32
 BANKS = 8
 LINE = 4
 BIAS_ROW = P - 1
-WIDTHS = (256, 128, 128)
-READERS = ("SSSS", "VSVS", "VSVS")
-STORES = ((1, 1, 1, 1,), (2, 2,), (2, 2,))
+WIDTHS = (128, 128, 128, 128)
+READERS = ("SSSS", "SSSS", "VSVS", "VSVS")
+STORES = ((2, 2,), (2, 2,), (2, 2,), (2, 2,))
 
 FLOPS = 2 * FEATURES * LISTED * QUERIES
 BYTES = 4 * FEATURES * QUERIES + (FEATURES + BLOCKS + 4) * NEURONS + 2 * P * LISTED // 16 + 4 * LISTED * QUERIES
@@ -42,12 +42,12 @@ def tile_attend_neut_relu_topk_kernel(tc, qT, k_words, k_scales, nb, offs, out):
         psum = ctx.enter_context(tc.psum_pool(name="psum", bufs=1))
 
         offsets = keep.tile([P, LISTED // 16], U16, name="offsets")
-        scale_table = keep.tile([P, NEURONS], U8, name="scale_table", tag="scales_then_codes", align_bytes=64)
+        scale_table = keep.tile([P, NEURONS], U8, name="scale_table", align_bytes=64)
         nc.vector.memset(scale_table[:].bitcast(I32), 0)
         identity = keep.tile([P, P], F32, name="identity")
         nc.vector.memset(identity[:], 0.0)
         make_identity(nc, identity[:], nomemset=True)
-        bias_table = keep.tile([P, NEURONS], F32, name="bias_table")
+        bias_table = keep.tile([P, NEURONS], F32, name="bias_table", tag="bias_then_codes", align_bytes=64)
         nc.vector.memset(bias_table[0:BIAS_ROW, :].bitcast(I32), 0)
         word_table = keep.tile([P, NEURONS], I32, name="word_table", align_bytes=64)
 
@@ -55,7 +55,7 @@ def tile_attend_neut_relu_topk_kernel(tc, qT, k_words, k_scales, nb, offs, out):
         starts = [sum(WIDTHS[:c]) for c in chunks]
         q_planes = qT[0].rearrange("(p t) q -> p t q", t=PACK)
         scale_rows = k_scales[0].bitcast(I32)
-        q_raw = [keep.tile([P, PACK, WIDTHS[c]], F32, name="q_raw%d" % c) for c in chunks]
+        q_raw = [keep.tile([P, PACK, WIDTHS[c]], F32, name="q_raw%d" % c, tag="raw%d" % c, align_bytes=64) for c in chunks]
 
         def load_queries(c, planes):
             nc.sync.dma_start(q_raw[c][:, planes, :], q_planes[:, planes, starts[c] : starts[c] + WIDTHS[c]])
@@ -72,17 +72,14 @@ def tile_attend_neut_relu_topk_kernel(tc, qT, k_words, k_scales, nb, offs, out):
         load_queries(0, first_parts[0])
         for r in range(4):
             nc.sync.dma_start(scale_table[r:P:QUADRANT, :].bitcast(I32), scale_rows[r:BLOCKS:4, :])
-        for planes in first_parts[1:]:
-            load_queries(0, planes)
         load_words()
         for c in chunks[1:]:
             load_queries(c, slice(0, PACK))
 
         grouped, q_scales, q_codes, result = [], [], [None for c in chunks], []
         for c in chunks:
-            grouped.append(keep.tile([P, WIDTHS[c], PACK], BF16, name="grouped%d" % c, align_bytes=64))
+            grouped.append(keep.tile([P, WIDTHS[c], PACK], BF16, name="grouped", tag="grouped%d" % c, align_bytes=64))
             q_scales.append(keep.tile([P, WIDTHS[c]], U8, name="q_scales%d" % c, align_bytes=64))
-            result.append(keep.tile([P, TILES, WIDTHS[c]], F32, name="result%d" % c))
 
         def interleave(engine, c, rows, planes):
             dst = grouped[c][:, rows, planes].rearrange("p (c i) t -> p c t i", i=LINE)
@@ -114,7 +111,7 @@ def tile_attend_neut_relu_topk_kernel(tc, qT, k_words, k_scales, nb, offs, out):
         k_scale = keep.tile([P, LISTED], U8, name="k_scale", align_bytes=64)
         nc.vector.tensor_copy(k_scale[:], scale_table[:].indirect(offsets[:]))
 
-        quantise(0, "scales_then_codes")
+        quantise(0, "bias_then_codes")
 
         k_codes = []
         for g in range(2):
@@ -125,9 +122,13 @@ def tile_attend_neut_relu_topk_kernel(tc, qT, k_words, k_scales, nb, offs, out):
         interleave("V", 2, slice(0, 128), slice(0, PACK))
         quantise(1, "codes1")
         quantise(2, "codes2")
+        interleave("V", 3, slice(0, 128), slice(0, PACK))
+        quantise(3, "codes3")
 
         out_tiles = out[0].rearrange("(j p) q -> p j q", p=P)
         for c in chunks:
+            tag = {0: "raw1", 2: "grouped3"}.get(c, "result%d" % c)
+            result.append(keep.tile([P, TILES, WIDTHS[c]], F32, name="result", tag=tag, align_bytes=64))
             stored = 0
             ends = [sum(STORES[c][: n + 1]) for n in range(len(STORES[c]))]
             for j in range(TILES):

@@ -27,6 +27,8 @@ QUADRANT = 32
 BANKS = 8
 LINE = 4
 BIAS_ROW = P - 1
+SCALE_ROW = P - BLOCKS
+RAW_BYTES = 4 * PACK * 128
 WIDTHS = (128, 128, 128, 128)
 READERS = ("SSSS", "SSSS", "VSVS", "VSVS")
 STORES = ((2, 2,), (2, 2,), (2, 2,), (2, 2,))
@@ -39,11 +41,14 @@ def tile_attend_neut_relu_topk_kernel(tc, qT, k_words, k_scales, nb, offs, out):
     nc = tc.nc
     with ExitStack() as ctx:
         keep = ctx.enter_context(tc.tile_pool(name="keep", bufs=1))
+        shared = ctx.enter_context(tc.tile_pool(name="shared", bufs=1))
         psum = ctx.enter_context(tc.psum_pool(name="psum", bufs=1))
 
         offsets = keep.tile([P, LISTED // 16], U16, name="offsets")
-        scale_table = keep.tile([P, NEURONS], U8, name="scale_table", align_bytes=64)
-        nc.vector.memset(scale_table[:].bitcast(I32), 0)
+        scale_table = shared.tile([P, NEURONS], U8, name="scale_table", align_bytes=64, offset=RAW_BYTES // 2)
+        nc.vector.memset(scale_table[0:SCALE_ROW, :].bitcast(I32), 0)
+        k_scale = keep.tile([P, LISTED], U8, name="k_scale", align_bytes=64)
+        nc.vector.memset(k_scale[:].bitcast(I32), 0)
         identity = keep.tile([P, P], F32, name="identity")
         nc.vector.memset(identity[:], 0.0)
         make_identity(nc, identity[:], nomemset=True)
@@ -55,7 +60,7 @@ def tile_attend_neut_relu_topk_kernel(tc, qT, k_words, k_scales, nb, offs, out):
         starts = [sum(WIDTHS[:c]) for c in chunks]
         q_planes = qT[0].rearrange("(p t) q -> p t q", t=PACK)
         scale_rows = k_scales[0].bitcast(I32)
-        q_raw = [keep.tile([P, PACK, WIDTHS[c]], F32, name="q_raw%d" % c, tag="raw%d" % c, align_bytes=64) for c in chunks]
+        q_raw = [keep.tile([P, PACK, WIDTHS[c]], F32, name="q_raw%d" % c, tag="raw%d" % c, align_bytes=64) for c in (0, 1)]
 
         def load_queries(c, planes):
             nc.sync.dma_start(q_raw[c][:, planes, :], q_planes[:, planes, starts[c] : starts[c] + WIDTHS[c]])
@@ -68,12 +73,20 @@ def tile_attend_neut_relu_topk_kernel(tc, qT, k_words, k_scales, nb, offs, out):
 
         first_parts = [slice(0, PACK)]
         nc.sync.dma_start(offsets[:], offs)
+        nc.sync.dma_start(scale_table[SCALE_ROW:P, :].bitcast(I32), scale_rows)
         load_bias_row()
         load_queries(0, first_parts[0])
-        for r in range(4):
-            nc.sync.dma_start(scale_table[r:P:QUADRANT, :].bitcast(I32), scale_rows[r:BLOCKS:4, :])
         load_words()
-        for c in chunks[1:]:
+        load_queries(1, slice(0, PACK))
+
+        scale_listed = keep.tile([P, LISTED], U8, name="scale_listed", align_bytes=64)
+        nc.vector.tensor_copy(scale_listed[:], scale_table[:].indirect(offsets[:]))
+        for r in range(4):
+            nc.sync.dma_start(k_scale[r:P:QUADRANT, :].bitcast(I32), scale_listed[SCALE_ROW + r : P : 4, :].bitcast(I32))
+        for c in (2, 3):
+            q_raw.append(
+                shared.tile([P, PACK, WIDTHS[c]], F32, name="q_raw%d" % c, align_bytes=64, offset=(c - 2) * RAW_BYTES)
+            )
             load_queries(c, slice(0, PACK))
 
         grouped, q_scales, q_codes, result = [], [], [None for c in chunks], []
@@ -107,9 +120,6 @@ def tile_attend_neut_relu_topk_kernel(tc, qT, k_words, k_scales, nb, offs, out):
             nc.tensor.transpose(turned[:, j, :], bias_listed[:, j * P : (j + 1) * P], identity[:])
         bias = keep.tile([P, TILES], F32, name="bias")
         nc.scalar.copy(bias[:], turned[:, :, BIAS_ROW])
-
-        k_scale = keep.tile([P, LISTED], U8, name="k_scale", align_bytes=64)
-        nc.vector.tensor_copy(k_scale[:], scale_table[:].indirect(offsets[:]))
 
         quantise(0, "bias_then_codes")
 

@@ -30,8 +30,7 @@ BIAS_ROW = P - 1
 SCALE_ROW = P - BLOCKS
 RAW_BYTES = 4 * PACK * 128
 WIDTHS = (128, 128, 128, 128)
-READERS = ("SSSS", "SSSS", "VSVS", "VSVS")
-STORES = ((2, 2,), (2, 2,), (2, 2,), (2, 2,))
+PAIR = 2
 
 FLOPS = 2 * FEATURES * LISTED * QUERIES
 BYTES = 4 * FEATURES * QUERIES + (FEATURES + BLOCKS + 4) * NEURONS + 2 * P * LISTED // 16 + 4 * LISTED * QUERIES
@@ -89,10 +88,12 @@ def tile_attend_neut_relu_topk_kernel(tc, qT, k_words, k_scales, nb, offs, out):
             )
             load_queries(c, slice(0, PACK))
 
-        grouped, q_scales, q_codes, result = [], [], [None for c in chunks], []
+        grouped, q_scales, q_codes = [], [], [None for c in chunks]
         for c in chunks:
-            grouped.append(keep.tile([P, WIDTHS[c], PACK], BF16, name="grouped", tag="grouped%d" % c, align_bytes=64))
             q_scales.append(keep.tile([P, WIDTHS[c]], U8, name="q_scales%d" % c, align_bytes=64))
+
+        def interleaved_tile(c, tag):
+            grouped.append(keep.tile([P, WIDTHS[c], PACK], BF16, name="grouped", tag=tag, align_bytes=64))
 
         def interleave(engine, c, rows, planes):
             dst = grouped[c][:, rows, planes].rearrange("p (c i) t -> p c t i", i=LINE)
@@ -110,6 +111,7 @@ def tile_attend_neut_relu_topk_kernel(tc, qT, k_words, k_scales, nb, offs, out):
                 in_=grouped[c][:].rearrange("p c t -> p (c t)"),
             )
 
+        interleaved_tile(0, "grouped0")
         for planes in first_parts:
             interleave("S", 0, slice(0, WIDTHS[0]), planes)
 
@@ -128,36 +130,46 @@ def tile_attend_neut_relu_topk_kernel(tc, qT, k_words, k_scales, nb, offs, out):
             k_codes.append(keep.tile([P, 2 * P], U32, name="k_codes%d" % g, align_bytes=64))
             nc.vector.tensor_copy(k_codes[g][:], word_table[:].bitcast(U32).indirect(offsets[:, 16 * g : 16 * (g + 1)]))
 
-        interleave("S", 1, slice(0, 128), slice(0, PACK))
-        interleave("V", 2, slice(0, 128), slice(0, PACK))
-        quantise(1, "codes1")
-        quantise(2, "codes2")
-        interleave("V", 3, slice(0, 128), slice(0, PACK))
-        quantise(3, "codes3")
-
         out_tiles = out[0].rearrange("(j p) q -> p j q", p=P)
-        for c in chunks:
-            tag = {0: "raw1", 2: "grouped3"}.get(c, "result%d" % c)
-            result.append(keep.tile([P, TILES, WIDTHS[c]], F32, name="result", tag=tag, align_bytes=64))
-            stored = 0
-            ends = [sum(STORES[c][: n + 1]) for n in range(len(STORES[c]))]
-            for j in range(TILES):
+
+        def multiply(c, pair, readers, result):
+            for n in range(PAIR):
+                j = PAIR * pair + n
                 acc = psum.tile([P, WIDTHS[c]], F32, name="acc", tag="bank%d" % ((TILES * c + j) % BANKS))
                 nc.tensor.matmul_mx(
                     out=acc[:],
-                    lhsT=k_codes[j // 2][:, (j % 2) * P : (j % 2 + 1) * P].bitcast(FP8X4),
+                    lhsT=k_codes[pair][:, n * P : (n + 1) * P].bitcast(FP8X4),
                     lhsT_scale=k_scale[:, j * P : (j + 1) * P],
                     rhs=q_codes[c][:].bitcast(FP8X4),
                     rhs_scale=q_scales[c][:],
                     start=True,
                     stop=True,
                 )
-                if READERS[c][j] == "S":
-                    nc.scalar.activation(result[c][:, j, :], acc[:], RELU, bias=bias[:, j : j + 1])
+                if readers[n] == "S":
+                    nc.scalar.activation(result[:, n, :], acc[:], RELU, bias=bias[:, j : j + 1])
                 else:
-                    nc.vector.tensor_scalar(result[c][:, j, :], acc[:], bias[:, j : j + 1], 0.0, ADD, MAX)
-                if j + 1 in ends:
-                    nc.sync.dma_start(
-                        out_tiles[:, stored : j + 1, starts[c] : starts[c] + WIDTHS[c]], result[c][:, stored : j + 1, :]
-                    )
-                    stored = j + 1
+                    nc.vector.tensor_scalar(result[:, n, :], acc[:], bias[:, j : j + 1], 0.0, ADD, MAX)
+            nc.sync.dma_start(
+                out_tiles[:, PAIR * pair : PAIR * (pair + 1), starts[c] : starts[c] + WIDTHS[c]], result[:]
+            )
+
+        def result_tile(c, tag):
+            return keep.tile([P, PAIR, WIDTHS[c]], F32, name="result", tag=tag, align_bytes=64)
+
+        interleaved_tile(1, "grouped1")
+        interleave("S", 1, slice(0, 128), slice(0, PACK))
+        quantise(1, "codes1")
+        multiply(0, 0, "SS", result_tile(0, "raw1"))
+        multiply(0, 1, "SS", result_tile(0, "result01"))
+        interleaved_tile(2, "grouped2")
+        interleave("V", 2, slice(0, 128), slice(0, PACK))
+        quantise(2, "codes2")
+        multiply(1, 0, "SS", result_tile(1, "result10"))
+        multiply(1, 1, "SS", result_tile(1, "result11"))
+        interleaved_tile(3, "grouped3")
+        interleave("V", 3, slice(0, 128), slice(0, PACK))
+        quantise(3, "codes3")
+        multiply(2, 0, "VS", result_tile(2, "grouped3"))
+        multiply(2, 1, "VS", result_tile(2, "result21"))
+        multiply(3, 0, "VS", result_tile(3, "result30"))
+        multiply(3, 1, "VS", result_tile(3, "result31"))

@@ -65,7 +65,7 @@ def tile_attend_neut_relu_topk_kernel(tc, qT, k_words, k_scales, nb, offs, out):
             nc.sync.dma_start(q_raw[c][:, planes, :], q_planes[:, planes, starts[c] : starts[c] + WIDTHS[c]])
 
         def load_bias_row():
-            nc.sync.dma_start(bias_table[BIAS_ROW : BIAS_ROW + 1, :], nb[BIAS_ROW : BIAS_ROW + 1, :])
+            nc.scalar.dma_start(bias_table[BIAS_ROW : BIAS_ROW + 1, :], nb[BIAS_ROW : BIAS_ROW + 1, :])
 
         def load_words():
             nc.sync.dma_start(word_table[:], k_words[0].rearrange("p n r -> p (n r)").bitcast(I32))
@@ -150,11 +150,11 @@ def tile_attend_neut_relu_topk_kernel(tc, qT, k_words, k_scales, nb, offs, out):
                 else:
                     nc.vector.tensor_scalar(result[:, n, :], acc[:], bias[:, j : j + 1], 0.0, ADD, MAX)
             nc.sync.dma_start(
-                out_tiles[:, PAIR * pair : PAIR * (pair + 1), starts[c] : starts[c] + WIDTHS[c]], result[:]
+                out_tiles[:, PAIR * pair : PAIR * (pair + 1), starts[c] : starts[c] + WIDTHS[c]], result
             )
 
         def result_tile(c, tag):
-            return keep.tile([P, PAIR, WIDTHS[c]], F32, name="result", tag=tag, align_bytes=64)
+            return keep.tile([P, PAIR, WIDTHS[c]], F32, name="result", tag=tag, align_bytes=64)[:]
 
         interleaved_tile(1, "grouped1")
         interleave("S", 1, slice(0, 128), slice(0, PACK))
@@ -169,7 +169,8 @@ def tile_attend_neut_relu_topk_kernel(tc, qT, k_words, k_scales, nb, offs, out):
         interleaved_tile(3, "grouped3")
         interleave("V", 3, slice(0, 128), slice(0, PACK))
         quantise(3, "codes3")
-        multiply(2, 0, "VS", result_tile(2, "grouped3"))
-        multiply(2, 1, "VS", result_tile(2, "result21"))
+        result2 = keep.tile([P, TILES, WIDTHS[2]], F32, name="result2", tag="grouped3", align_bytes=64)
+        multiply(2, 0, "VS", result2[:, 0:PAIR, :])
+        multiply(2, 1, "VS", result2[:, PAIR:TILES, :])
         multiply(3, 0, "VS", result_tile(3, "result30"))
         multiply(3, 1, "VS", result_tile(3, "result31"))

@@ -72,7 +72,7 @@ def tile_attend_neut_relu_topk_kernel(tc, qT, k_words, k_scales, nb, offs, out):
 
         first_parts = [slice(0, PACK)]
         nc.sync.dma_start(offsets[:], offs)
-        nc.sync.dma_start(scale_table[SCALE_ROW:P, :].bitcast(I32), scale_rows)
+        nc.scalar.dma_start(scale_table[SCALE_ROW:P, :].bitcast(I32), scale_rows)
         load_bias_row()
         load_queries(0, first_parts[0])
         load_words()

@@ -81,7 +81,7 @@ def tile_attend_neut_relu_topk_kernel(tc, qT, k_words, k_scales, nb, offs, out):
         scale_listed = keep.tile([P, LISTED], U8, name="scale_listed", align_bytes=64)
         nc.vector.tensor_copy(scale_listed[:], scale_table[:].indirect(offsets[:]))
         for r in range(4):
-            nc.sync.dma_start(k_scale[r:P:QUADRANT, :].bitcast(I32), scale_listed[SCALE_ROW + r : P : 4, :].bitcast(I32))
+            (nc.sync, nc.scalar)[r % 2].dma_start(k_scale[r:P:QUADRANT, :].bitcast(I32), scale_listed[SCALE_ROW + r : P : 4, :].bitcast(I32))
         for c in (2, 3):
             q_raw.append(
                 shared.tile([P, PACK, WIDTHS[c]], F32, name="q_raw%d" % c, align_bytes=64, offset=(c - 2) * RAW_BYTES)

@@ -126,9 +126,10 @@ def tile_attend_neut_relu_topk_kernel(tc, qT, k_words, k_scales, nb, offs, out):
         quantise(0, "bias_then_codes")
 
         k_codes = []
-        for g in range(2):
-            k_codes.append(keep.tile([P, 2 * P], U32, name="k_codes%d" % g, align_bytes=64))
-            nc.vector.tensor_copy(k_codes[g][:], word_table[:].bitcast(U32).indirect(offsets[:, 16 * g : 16 * (g + 1)]))
+        for first, count in ((0, 2), (2, 1), (3, 1)):
+            part = keep.tile([P, count * P], U32, name="k_codes%d" % first, align_bytes=64)
+            nc.vector.tensor_copy(part[:], word_table[:].bitcast(U32).indirect(offsets[:, 8 * first : 8 * (first + count)]))
+            k_codes.extend(part[:, n * P : (n + 1) * P] for n in range(count))
 
         out_tiles = out[0].rearrange("(j p) q -> p j q", p=P)
 
@@ -138,7 +139,7 @@ def tile_attend_neut_relu_topk_kernel(tc, qT, k_words, k_scales, nb, offs, out):
                 acc = psum.tile([P, WIDTHS[c]], F32, name="acc", tag="bank%d" % ((TILES * c + j) % BANKS))
                 nc.tensor.matmul_mx(
                     out=acc[:],
-                    lhsT=k_codes[pair][:, n * P : (n + 1) * P].bitcast(FP8X4),
+                    lhsT=k_codes[j].bitcast(FP8X4),
                     lhsT_scale=k_scale[:, j * P : (j + 1) * P],
                     rhs=q_codes[c][:].bitcast(FP8X4),
                     rhs_scale=q_scales[c][:],

@@ -44,13 +44,13 @@ def tile_attend_neut_relu_topk_kernel(tc, qT, k_words, k_scales, nb, offs, out):
         psum = ctx.enter_context(tc.psum_pool(name="psum", bufs=1))
 
         offsets = keep.tile([P, LISTED // 16], U16, name="offsets")
+        identity = keep.tile([P, P], F32, name="identity")
+        nc.vector.memset(identity[:], 0.0)
+        make_identity(nc, identity[:], nomemset=True)
         scale_table = shared.tile([P, NEURONS], U8, name="scale_table", align_bytes=64, offset=RAW_BYTES // 2)
         nc.vector.memset(scale_table[0:SCALE_ROW, :].bitcast(I32), 0)
         k_scale = keep.tile([P, LISTED], U8, name="k_scale", align_bytes=64)
         nc.vector.memset(k_scale[:].bitcast(I32), 0)
-        identity = keep.tile([P, P], F32, name="identity")
-        nc.vector.memset(identity[:], 0.0)
-        make_identity(nc, identity[:], nomemset=True)
         bias_table = keep.tile([P, NEURONS], F32, name="bias_table", tag="bias_then_codes", align_bytes=64)
         nc.vector.memset(bias_table[0:BIAS_ROW, :].bitcast(I32), 0)
         word_table = keep.tile([P, NEURONS], I32, name="word_table", align_bytes=64)
@@ -59,7 +59,10 @@ def tile_attend_neut_relu_topk_kernel(tc, qT, k_words, k_scales, nb, offs, out):
         starts = [sum(WIDTHS[:c]) for c in chunks]
         q_planes = qT[0].rearrange("(p t) q -> p t q", t=PACK)
         scale_rows = k_scales[0].bitcast(I32)
-        q_raw = [keep.tile([P, PACK, WIDTHS[c]], F32, name="q_raw%d" % c, tag="raw%d" % c, align_bytes=64) for c in (0, 1)]
+        q_raw = [
+            keep.tile([P, PACK, WIDTHS[0]], F32, name="q_raw0", align_bytes=64),
+            shared.tile([P, PACK, WIDTHS[1]], F32, name="q_raw1", align_bytes=64, offset=2 * RAW_BYTES),
+        ]
 
         def load_queries(c, planes):
             nc.sync.dma_start(q_raw[c][:, planes, :], q_planes[:, planes, starts[c] : starts[c] + WIDTHS[c]])
@@ -115,13 +118,15 @@ def tile_attend_neut_relu_topk_kernel(tc, qT, k_words, k_scales, nb, offs, out):
         for planes in first_parts:
             interleave("S", 0, slice(0, WIDTHS[0]), planes)
 
-        bias_listed = keep.tile([P, LISTED], F32, name="bias_listed")
-        nc.vector.tensor_copy(bias_listed[:], bias_table[:].indirect(offsets[:]))
-        turned = psum.tile([P, TILES, P], F32, name="turned", tag="bank%d" % (BANKS - 1))
-        for j in range(TILES):
-            nc.tensor.transpose(turned[:, j, :], bias_listed[:, j * P : (j + 1) * P], identity[:])
-        bias = keep.tile([P, TILES], F32, name="bias")
-        nc.scalar.copy(bias[:], turned[:, :, BIAS_ROW])
+        bias, turned = [], []
+        for g in range(2):
+            bias_listed = keep.tile([P, PAIR * P], F32, name="bias_listed", tag=("grouped1", "listed1")[g], align_bytes=64)
+            nc.vector.tensor_copy(bias_listed[:], bias_table[:].indirect(offsets[:, 16 * g : 16 * (g + 1)]))
+            turned.append(psum.tile([P, PAIR, P], F32, name="turned", tag="bank%d" % (BANKS - 2 + g)))
+            for n in range(PAIR):
+                nc.tensor.transpose(turned[g][:, n, :], bias_listed[:, n * P : (n + 1) * P], identity[:])
+            bias.append(keep.tile([P, PAIR], F32, name="bias%d" % g))
+        nc.scalar.copy(bias[0][:], turned[0][:, :, BIAS_ROW])
 
         quantise(0, "bias_then_codes")
 
@@ -147,9 +152,9 @@ def tile_attend_neut_relu_topk_kernel(tc, qT, k_words, k_scales, nb, offs, out):
                     stop=True,
                 )
                 if readers[n] == "S":
-                    nc.scalar.activation(result[:, n, :], acc[:], RELU, bias=bias[:, j : j + 1])
+                    nc.scalar.activation(result[:, n, :], acc[:], RELU, bias=bias[pair][:, n : n + 1])
                 else:
-                    nc.vector.tensor_scalar(result[:, n, :], acc[:], bias[:, j : j + 1], 0.0, ADD, MAX)
+                    nc.vector.tensor_scalar(result[:, n, :], acc[:], bias[pair][:, n : n + 1], 0.0, ADD, MAX)
             nc.sync.dma_start(
                 out_tiles[:, PAIR * pair : PAIR * (pair + 1), starts[c] : starts[c] + WIDTHS[c]], result
             )
@@ -159,18 +164,22 @@ def tile_attend_neut_relu_topk_kernel(tc, qT, k_words, k_scales, nb, offs, out):
 
         interleaved_tile(1, "grouped1")
         interleave("S", 1, slice(0, 128), slice(0, PACK))
+        nc.scalar.copy(bias[1][:], turned[1][:, :, BIAS_ROW])
         quantise(1, "codes1")
-        multiply(0, 0, "SS", result_tile(0, "raw1"))
+        result0 = shared.tile([P, PAIR, WIDTHS[0]], F32, name="result0", align_bytes=64, offset=2 * RAW_BYTES)
+        multiply(0, 0, "SS", result0[:])
         multiply(0, 1, "SS", result_tile(0, "result01"))
-        interleaved_tile(2, "grouped2")
+        grouped.append(
+            shared.tile([P, WIDTHS[2], PACK], BF16, name="grouped2", align_bytes=64, offset=5 * RAW_BYTES // 2)
+        )
         interleave("V", 2, slice(0, 128), slice(0, PACK))
         quantise(2, "codes2")
         multiply(1, 0, "SS", result_tile(1, "result10"))
         multiply(1, 1, "SS", result_tile(1, "result11"))
-        interleaved_tile(3, "grouped3")
+        grouped.append(shared.tile([P, WIDTHS[3], PACK], BF16, name="grouped3", align_bytes=64, offset=0))
         interleave("V", 3, slice(0, 128), slice(0, PACK))
         quantise(3, "codes3")
-        result2 = keep.tile([P, TILES, WIDTHS[2]], F32, name="result2", tag="grouped3", align_bytes=64)
+        result2 = shared.tile([P, TILES, WIDTHS[2]], F32, name="result2", align_bytes=64, offset=0)
         multiply(2, 0, "VS", result2[:, 0:PAIR, :])
         multiply(2, 1, "VS", result2[:, PAIR:TILES, :])
         multiply(3, 0, "VS", result_tile(3, "result30"))

@@ -51,7 +51,7 @@ def tile_attend_neut_relu_topk_kernel(tc, qT, k_words, k_scales, nb, offs, out):
         nc.vector.memset(scale_table[0:SCALE_ROW, :].bitcast(I32), 0)
         k_scale = keep.tile([P, LISTED], U8, name="k_scale", align_bytes=64)
         nc.vector.memset(k_scale[:].bitcast(I32), 0)
-        bias_table = keep.tile([P, NEURONS], F32, name="bias_table", tag="bias_then_codes", align_bytes=64)
+        bias_table = keep.tile([P, NEURONS], F32, name="bias_table", tag="bias_table", align_bytes=64)
         nc.vector.memset(bias_table[0:BIAS_ROW, :].bitcast(I32), 0)
         word_table = keep.tile([P, NEURONS], I32, name="word_table", align_bytes=64)
 
@@ -128,7 +128,7 @@ def tile_attend_neut_relu_topk_kernel(tc, qT, k_words, k_scales, nb, offs, out):
             bias.append(keep.tile([P, PAIR], F32, name="bias%d" % g))
         nc.scalar.copy(bias[0][:], turned[0][:, :, BIAS_ROW])
 
-        quantise(0, "bias_then_codes")
+        quantise(0, "codes0")
 
         k_codes = []
         for first, count in ((0, 2), (2, 1), (3, 1)):
@@ -168,11 +168,11 @@ def tile_attend_neut_relu_topk_kernel(tc, qT, k_words, k_scales, nb, offs, out):
         quantise(1, "codes1")
         result0 = shared.tile([P, PAIR, WIDTHS[0]], F32, name="result0", align_bytes=64, offset=2 * RAW_BYTES)
         multiply(0, 0, "SS", result0[:])
-        multiply(0, 1, "SS", result_tile(0, "result01"))
         grouped.append(
             shared.tile([P, WIDTHS[2], PACK], BF16, name="grouped2", align_bytes=64, offset=5 * RAW_BYTES // 2)
         )
         interleave("V", 2, slice(0, 128), slice(0, PACK))
+        multiply(0, 1, "VS", result_tile(0, "grouped1"))
         quantise(2, "codes2")
         multiply(1, 0, "SS", result_tile(1, "result10"))
         multiply(1, 1, "SS", result_tile(1, "result11"))

@@ -166,8 +166,7 @@ def tile_attend_neut_relu_topk_kernel(tc, qT, k_words, k_scales, nb, offs, out):
         interleave("S", 1, slice(0, 128), slice(0, PACK))
         nc.scalar.copy(bias[1][:], turned[1][:, :, BIAS_ROW])
         quantise(1, "codes1")
-        result0 = shared.tile([P, PAIR, WIDTHS[0]], F32, name="result0", align_bytes=64, offset=2 * RAW_BYTES)
-        multiply(0, 0, "SS", result0[:])
+        multiply(0, 0, "SS", result_tile(0, "result00"))
         grouped.append(
             shared.tile([P, WIDTHS[2], PACK], BF16, name="grouped2", align_bytes=64, offset=5 * RAW_BYTES // 2)
         )
@@ -179,7 +178,7 @@ def tile_attend_neut_relu_topk_kernel(tc, qT, k_words, k_scales, nb, offs, out):
         grouped.append(shared.tile([P, WIDTHS[3], PACK], BF16, name="grouped3", align_bytes=64, offset=0))
         interleave("V", 3, slice(0, 128), slice(0, PACK))
         quantise(3, "codes3")
-        result2 = shared.tile([P, TILES, WIDTHS[2]], F32, name="result2", align_bytes=64, offset=0)
+        result2 = shared.tile([P, TILES, WIDTHS[2]], F32, name="result2", align_bytes=64, offset=RAW_BYTES)
         multiply(2, 0, "VS", result2[:, 0:PAIR, :])
         multiply(2, 1, "VS", result2[:, PAIR:TILES, :])
         multiply(3, 0, "VS", result_tile(3, "result30"))

@@ -24,16 +24,18 @@ QUERIES = 512
 TILES = LISTED // P
 BLOCKS = FEATURES // 32
 QUADRANT = 32
+GROUP = 16
 BANKS = 8
 LINE = 4
 BIAS_ROW = P - 1
 SCALE_ROW = P - BLOCKS
-RAW_BYTES = 4 * PACK * 128
-WIDTHS = (128, 128, 128, 128)
+CHUNK = 128
+CHUNKS = QUERIES // CHUNK
+RAW_BYTES = 4 * PACK * CHUNK
 PAIR = 2
 
 FLOPS = 2 * FEATURES * LISTED * QUERIES
-BYTES = 4 * FEATURES * QUERIES + (FEATURES + BLOCKS + 4) * NEURONS + 2 * P * LISTED // 16 + 4 * LISTED * QUERIES
+BYTES = 4 * FEATURES * QUERIES + (FEATURES + BLOCKS + 4) * NEURONS + 2 * P * LISTED // GROUP + 4 * LISTED * QUERIES
 
 
 def tile_attend_neut_relu_topk_kernel(tc, qT, k_words, k_scales, nb, offs, out):
@@ -43,97 +45,94 @@ def tile_attend_neut_relu_topk_kernel(tc, qT, k_words, k_scales, nb, offs, out):
         shared = ctx.enter_context(tc.tile_pool(name="shared", bufs=1))
         psum = ctx.enter_context(tc.psum_pool(name="psum", bufs=1))
 
-        offsets = keep.tile([P, LISTED // 16], U16, name="offsets")
+        def placed(shape, dtype, name, offset):
+            return shared.tile(shape, dtype, name=name, align_bytes=64, offset=offset)
+
+        raw_at = {1: 2 * RAW_BYTES, 2: 0, 3: RAW_BYTES}
+
+        offsets = keep.tile([P, LISTED // GROUP], U16, name="offsets")
+
+        def listed(table, first, count):
+            return table.indirect(offsets[:, first * P // GROUP : (first + count) * P // GROUP])
+
         identity = keep.tile([P, P], F32, name="identity")
         nc.vector.memset(identity[:], 0.0)
         make_identity(nc, identity[:], nomemset=True)
-        scale_table = shared.tile([P, NEURONS], U8, name="scale_table", align_bytes=64, offset=RAW_BYTES // 2)
+        scale_table = placed([P, NEURONS], U8, "scale_table", RAW_BYTES // 2)
         nc.vector.memset(scale_table[0:SCALE_ROW, :].bitcast(I32), 0)
         k_scale = keep.tile([P, LISTED], U8, name="k_scale", align_bytes=64)
         nc.vector.memset(k_scale[:].bitcast(I32), 0)
-        bias_table = keep.tile([P, NEURONS], F32, name="bias_table", tag="bias_table", align_bytes=64)
+        bias_table = keep.tile([P, NEURONS], F32, name="bias_table", align_bytes=64)
         nc.vector.memset(bias_table[0:BIAS_ROW, :].bitcast(I32), 0)
         word_table = keep.tile([P, NEURONS], I32, name="word_table", align_bytes=64)
 
-        chunks = range(len(WIDTHS))
-        starts = [sum(WIDTHS[:c]) for c in chunks]
         q_planes = qT[0].rearrange("(p t) q -> p t q", t=PACK)
-        scale_rows = k_scales[0].bitcast(I32)
-        q_raw = [
-            keep.tile([P, PACK, WIDTHS[0]], F32, name="q_raw0", align_bytes=64),
-            shared.tile([P, PACK, WIDTHS[1]], F32, name="q_raw1", align_bytes=64, offset=2 * RAW_BYTES),
-        ]
+        q_raw = [keep.tile([P, PACK, CHUNK], F32, name="q_raw0", align_bytes=64)]
 
-        def load_queries(c, planes):
-            nc.sync.dma_start(q_raw[c][:, planes, :], q_planes[:, planes, starts[c] : starts[c] + WIDTHS[c]])
+        def load_chunk(c):
+            if c > 0:
+                q_raw.append(placed([P, PACK, CHUNK], F32, "q_raw%d" % c, raw_at[c]))
+            nc.sync.dma_start(q_raw[c][:], q_planes[:, :, c * CHUNK : (c + 1) * CHUNK])
 
-        def load_bias_row():
-            nc.scalar.dma_start(bias_table[BIAS_ROW : BIAS_ROW + 1, :], nb[BIAS_ROW : BIAS_ROW + 1, :])
-
-        def load_words():
-            nc.sync.dma_start(word_table[:], k_words[0].rearrange("p n r -> p (n r)").bitcast(I32))
-
-        first_parts = [slice(0, PACK)]
         nc.sync.dma_start(offsets[:], offs)
-        nc.scalar.dma_start(scale_table[SCALE_ROW:P, :].bitcast(I32), scale_rows)
-        load_bias_row()
-        load_queries(0, first_parts[0])
-        load_words()
-        load_queries(1, slice(0, PACK))
+        nc.scalar.dma_start(scale_table[SCALE_ROW:P, :].bitcast(I32), k_scales[0].bitcast(I32))
+        nc.scalar.dma_start(bias_table[BIAS_ROW:P, :], nb[BIAS_ROW:P, :])
+        load_chunk(0)
+        nc.sync.dma_start(word_table[:], k_words[0].rearrange("p n r -> p (n r)").bitcast(I32))
+        load_chunk(1)
 
         scale_listed = keep.tile([P, LISTED], U8, name="scale_listed", align_bytes=64)
-        nc.vector.tensor_copy(scale_listed[:], scale_table[:].indirect(offsets[:]))
+        nc.vector.tensor_copy(scale_listed[:], listed(scale_table[:], 0, TILES))
         for r in range(4):
-            (nc.sync, nc.scalar)[r % 2].dma_start(k_scale[r:P:QUADRANT, :].bitcast(I32), scale_listed[SCALE_ROW + r : P : 4, :].bitcast(I32))
-        for c in (2, 3):
-            q_raw.append(
-                shared.tile([P, PACK, WIDTHS[c]], F32, name="q_raw%d" % c, align_bytes=64, offset=(c - 2) * RAW_BYTES)
-            )
-            load_queries(c, slice(0, PACK))
+            queue = (nc.sync, nc.scalar)[r % 2]
+            queue.dma_start(k_scale[r:P:QUADRANT, :].bitcast(I32), scale_listed[SCALE_ROW + r : P : 4, :].bitcast(I32))
+        load_chunk(2)
+        load_chunk(3)
 
-        grouped, q_scales, q_codes = [], [], [None for c in chunks]
-        for c in chunks:
-            q_scales.append(keep.tile([P, WIDTHS[c]], U8, name="q_scales%d" % c, align_bytes=64))
+        grouped, q_codes = {}, {}
+        q_scales = [keep.tile([P, CHUNK], U8, name="q_scales%d" % c, align_bytes=64) for c in range(CHUNKS)]
 
-        def interleaved_tile(c, tag):
-            grouped.append(keep.tile([P, WIDTHS[c], PACK], BF16, name="grouped", tag=tag, align_bytes=64))
-
-        def interleave(engine, c, rows, planes):
-            dst = grouped[c][:, rows, planes].rearrange("p (c i) t -> p c t i", i=LINE)
-            src = q_raw[c][:, planes, rows].rearrange("p t (c i) -> p c t i", i=LINE)
+        def interleave(engine, c, first, last):
+            dst = grouped[c][:, first:last, :].rearrange("p (c i) t -> p c t i", i=LINE)
+            src = q_raw[c][:, :, first:last].rearrange("p t (c i) -> p c t i", i=LINE)
             if engine == "S":
                 nc.scalar.activation(dst, src, COPY)
             else:
                 nc.vector.tensor_copy(dst, src)
 
-        def quantise(c, tag):
-            q_codes[c] = keep.tile([P, WIDTHS[c]], U32, name="q_codes%d" % c, tag=tag, align_bytes=64)
+        def quantise(c):
+            q_codes[c] = keep.tile([P, CHUNK], U32, name="q_codes%d" % c, align_bytes=64)
             nc.vector.quantize_mx(
                 out=q_codes[c][:].bitcast(FP8X4),
                 scales=q_scales[c][:],
                 in_=grouped[c][:].rearrange("p c t -> p (c t)"),
             )
 
-        interleaved_tile(0, "grouped0")
-        for planes in first_parts:
-            interleave("S", 0, slice(0, WIDTHS[0]), planes)
+        grouped[0] = keep.tile([P, CHUNK, PACK], BF16, name="grouped0", align_bytes=64)
+        interleave("S", 0, 0, CHUNK)
 
         bias, turned = [], []
-        for g in range(2):
-            bias_listed = keep.tile([P, PAIR * P], F32, name="bias_listed", tag=("grouped1", "listed1")[g], align_bytes=64)
-            nc.vector.tensor_copy(bias_listed[:], bias_table[:].indirect(offsets[:, 16 * g : 16 * (g + 1)]))
-            turned.append(psum.tile([P, PAIR, P], F32, name="turned", tag="bank%d" % (BANKS - 2 + g)))
+        for pair in range(TILES // PAIR):
+            bias_listed = keep.tile([P, PAIR * P], F32, name="bias_listed", tag="listed%d" % pair, align_bytes=64)
+            if pair == 0:
+                nc.vector.tensor_copy(bias_listed[:], listed(bias_table[:], PAIR * pair, PAIR))
+            else:
+                nc.scalar.activation(bias_listed[:], listed(bias_table[:], PAIR * pair, PAIR), COPY)
+            turned.append(psum.tile([P, PAIR, P], F32, name="turned", tag="bank%d" % (BANKS - 2 + pair)))
             for n in range(PAIR):
-                nc.tensor.transpose(turned[g][:, n, :], bias_listed[:, n * P : (n + 1) * P], identity[:])
-            bias.append(keep.tile([P, PAIR], F32, name="bias%d" % g))
-        nc.scalar.copy(bias[0][:], turned[0][:, :, BIAS_ROW])
+                nc.tensor.transpose(turned[pair][:, n, :], bias_listed[:, n * P : (n + 1) * P], identity[:])
+            bias.append(keep.tile([P, PAIR], F32, name="bias%d" % pair))
 
-        quantise(0, "codes0")
+        def fetch_bias(pair):
+            nc.scalar.copy(bias[pair][:], turned[pair][:, :, BIAS_ROW])
+
+        fetch_bias(0)
+        quantise(0)
 
         k_codes = []
-        for first, count in ((0, 2), (2, 1), (3, 1)):
+        for first, count in ((0, PAIR), (PAIR, 1), (PAIR + 1, 1)):
             part = keep.tile([P, count * P], U32, name="k_codes%d" % first, align_bytes=64)
-            nc.vector.tensor_copy(part[:], word_table[:].bitcast(U32).indirect(offsets[:, 8 * first : 8 * (first + count)]))
+            nc.vector.tensor_copy(part[:], listed(word_table[:].bitcast(U32), first, count))
             k_codes.extend(part[:, n * P : (n + 1) * P] for n in range(count))
 
         out_tiles = out[0].rearrange("(j p) q -> p j q", p=P)
@@ -141,7 +140,7 @@ def tile_attend_neut_relu_topk_kernel(tc, qT, k_words, k_scales, nb, offs, out):
         def multiply(c, pair, readers, result):
             for n in range(PAIR):
                 j = PAIR * pair + n
-                acc = psum.tile([P, WIDTHS[c]], F32, name="acc", tag="bank%d" % ((TILES * c + j) % BANKS))
+                acc = psum.tile([P, CHUNK], F32, name="acc", tag="bank%d" % ((TILES * c + j) % BANKS))
                 nc.tensor.matmul_mx(
                     out=acc[:],
                     lhsT=k_codes[j].bitcast(FP8X4),
@@ -155,31 +154,27 @@ def tile_attend_neut_relu_topk_kernel(tc, qT, k_words, k_scales, nb, offs, out):
                     nc.scalar.activation(result[:, n, :], acc[:], RELU, bias=bias[pair][:, n : n + 1])
                 else:
                     nc.vector.tensor_scalar(result[:, n, :], acc[:], bias[pair][:, n : n + 1], 0.0, ADD, MAX)
-            nc.sync.dma_start(
-                out_tiles[:, PAIR * pair : PAIR * (pair + 1), starts[c] : starts[c] + WIDTHS[c]], result
-            )
+            nc.sync.dma_start(out_tiles[:, PAIR * pair : PAIR * (pair + 1), c * CHUNK : (c + 1) * CHUNK], result)
 
-        def result_tile(c, tag):
-            return keep.tile([P, PAIR, WIDTHS[c]], F32, name="result", tag=tag, align_bytes=64)[:]
+        def result_tile(tag):
+            return keep.tile([P, PAIR, CHUNK], F32, name="result", tag=tag, align_bytes=64)[:]
 
-        interleaved_tile(1, "grouped1")
-        interleave("S", 1, slice(0, 128), slice(0, PACK))
-        nc.scalar.copy(bias[1][:], turned[1][:, :, BIAS_ROW])
-        quantise(1, "codes1")
-        multiply(0, 0, "SS", result_tile(0, "result00"))
-        grouped.append(
-            shared.tile([P, WIDTHS[2], PACK], BF16, name="grouped2", align_bytes=64, offset=5 * RAW_BYTES // 2)
-        )
-        interleave("V", 2, slice(0, 128), slice(0, PACK))
-        multiply(0, 1, "VS", result_tile(0, "grouped1"))
-        quantise(2, "codes2")
-        multiply(1, 0, "SS", result_tile(1, "result10"))
-        multiply(1, 1, "SS", result_tile(1, "result11"))
-        grouped.append(shared.tile([P, WIDTHS[3], PACK], BF16, name="grouped3", align_bytes=64, offset=0))
-        interleave("V", 3, slice(0, 128), slice(0, PACK))
-        quantise(3, "codes3")
-        result2 = shared.tile([P, TILES, WIDTHS[2]], F32, name="result2", align_bytes=64, offset=RAW_BYTES)
-        multiply(2, 0, "VS", result2[:, 0:PAIR, :])
-        multiply(2, 1, "VS", result2[:, PAIR:TILES, :])
-        multiply(3, 0, "VS", result_tile(3, "result30"))
-        multiply(3, 1, "VS", result_tile(3, "result31"))
+        grouped[1] = keep.tile([P, CHUNK, PACK], BF16, name="grouped1", tag="listed0", align_bytes=64)
+        interleave("S", 1, 0, CHUNK)
+        fetch_bias(1)
+        quantise(1)
+        multiply(0, 0, "SS", result_tile("result00"))
+        grouped[2] = placed([P, CHUNK, PACK], BF16, "grouped2", raw_at[1] + RAW_BYTES // 2)
+        interleave("V", 2, 0, CHUNK)
+        multiply(0, 1, "VS", result_tile("listed0"))
+        quantise(2)
+        multiply(1, 0, "SS", result_tile("result10"))
+        grouped[3] = placed([P, CHUNK, PACK], BF16, "grouped3", raw_at[2])
+        interleave("V", 3, 0, CHUNK)
+        multiply(1, 1, "SS", result_tile("result11"))
+        quantise(3)
+        result2 = placed([P, TILES, CHUNK], F32, "result2", raw_at[3])
+        for pair in range(TILES // PAIR):
+            multiply(2, pair, "VS", result2[:, PAIR * pair : PAIR * (pair + 1), :])
+        for pair in range(TILES // PAIR):
+            multiply(3, pair, "VS", result_tile("result3%d" % pair))

@@ -13,6 +13,7 @@ FP8X4 = mybir.dt.float8_e4m3fn_x4
 COPY = mybir.ActivationFunctionType.Copy
 RELU = mybir.ActivationFunctionType.Relu
 ADD = mybir.AluOpType.add
+MULT = mybir.AluOpType.mult
 MAX = mybir.AluOpType.max
 
 P = 128
@@ -32,6 +33,7 @@ SCALE_ROW = P - BLOCKS
 CHUNK = 128
 CHUNKS = QUERIES // CHUNK
 RAW_BYTES = 4 * PACK * CHUNK
+SHARE = 48
 PAIR = 2
 
 FLOPS = 2 * FEATURES * LISTED * QUERIES
@@ -97,6 +99,8 @@ def tile_attend_neut_relu_topk_kernel(tc, qT, k_words, k_scales, nb, offs, out):
             src = q_raw[c][:, :, first:last].rearrange("p t (c i) -> p c t i", i=LINE)
             if engine == "S":
                 nc.scalar.activation(dst, src, COPY)
+            elif engine == "G":
+                nc.gpsimd.tensor_scalar(dst, src, 1.0, 0.0, MULT, ADD)
             else:
                 nc.vector.tensor_copy(dst, src)
 
@@ -160,7 +164,8 @@ def tile_attend_neut_relu_topk_kernel(tc, qT, k_words, k_scales, nb, offs, out):
             return keep.tile([P, PAIR, CHUNK], F32, name="result", tag=tag, align_bytes=64)[:]
 
         grouped[1] = keep.tile([P, CHUNK, PACK], BF16, name="grouped1", tag="listed0", align_bytes=64)
-        interleave("S", 1, 0, CHUNK)
+        interleave("S", 1, 0, CHUNK - SHARE)
+        interleave("G", 1, CHUNK - SHARE, CHUNK)
         fetch_bias(1)
         quantise(1)
         multiply(0, 0, "SS", result_tile("result00"))

@@ -141,7 +141,8 @@ def tile_attend_neut_relu_topk_kernel(tc, qT, k_words, k_scales, nb, offs, out):
 
         out_tiles = out[0].rearrange("(j p) q -> p j q", p=P)
 
-        def multiply(c, pair, readers, result):
+        def multiply(c, pair, readers, result, singly=False):
+            columns = slice(c * CHUNK, (c + 1) * CHUNK)
             for n in range(PAIR):
                 j = PAIR * pair + n
                 acc = psum.tile([P, CHUNK], F32, name="acc", tag="bank%d" % ((TILES * c + j) % BANKS))
@@ -158,7 +159,10 @@ def tile_attend_neut_relu_topk_kernel(tc, qT, k_words, k_scales, nb, offs, out):
                     nc.scalar.activation(result[:, n, :], acc[:], RELU, bias=bias[pair][:, n : n + 1])
                 else:
                     nc.vector.tensor_scalar(result[:, n, :], acc[:], bias[pair][:, n : n + 1], 0.0, ADD, MAX)
-            nc.sync.dma_start(out_tiles[:, PAIR * pair : PAIR * (pair + 1), c * CHUNK : (c + 1) * CHUNK], result)
+                if singly:
+                    nc.sync.dma_start(out_tiles[:, j, columns], result[:, n, :])
+            if not singly:
+                nc.sync.dma_start(out_tiles[:, PAIR * pair : PAIR * (pair + 1), columns], result)
 
         def result_tile(tag):
             return keep.tile([P, PAIR, CHUNK], F32, name="result", tag=tag, align_bytes=64)[:]
@@ -168,7 +172,7 @@ def tile_attend_neut_relu_topk_kernel(tc, qT, k_words, k_scales, nb, offs, out):
         interleave("G", 1, CHUNK - SHARE, CHUNK)
         fetch_bias(1)
         quantise(1)
-        multiply(0, 0, "SS", result_tile("result00"))
+        multiply(0, 0, "SS", result_tile("result00"), singly=True)
         grouped[2] = placed([P, CHUNK, PACK], BF16, "grouped2", raw_at[1] + RAW_BYTES // 2)
         interleave("V", 2, 0, CHUNK)
         multiply(0, 1, "VS", result_tile("listed0"))

@@ -180,7 +180,7 @@ def tile_attend_neut_relu_topk_kernel(tc, qT, k_words, k_scales, nb, offs, out):
         multiply(1, 0, "SS", result_tile("result10"))
         grouped[3] = placed([P, CHUNK, PACK], BF16, "grouped3", raw_at[2])
         interleave("V", 3, 0, CHUNK)
-        multiply(1, 1, "SS", result_tile("result11"))
+        multiply(1, 1, "VS", placed([P, PAIR, CHUNK], F32, "result11", raw_at[1] + RAW_BYTES // 2)[:])
         quantise(3)
         result2 = placed([P, TILES, CHUNK], F32, "result2", raw_at[3])
         for pair in range(TILES // PAIR):

from contextlib import ExitStack

import concourse.mybir as mybir
from concourse.masks import make_identity

F32 = mybir.dt.float32
BF16 = mybir.dt.bfloat16
I32 = mybir.dt.int32
U32 = mybir.dt.uint32
U16 = mybir.dt.uint16
U8 = mybir.dt.uint8
FP8X4 = mybir.dt.float8_e4m3fn_x4
COPY = mybir.ActivationFunctionType.Copy
RELU = mybir.ActivationFunctionType.Relu
ADD = mybir.AluOpType.add
MULT = mybir.AluOpType.mult
MAX = mybir.AluOpType.max

P = 128
PACK = 4
FEATURES = P * PACK
NEURONS = 2048
LISTED = 512
QUERIES = 512
TILES = LISTED // P
BLOCKS = FEATURES // 32
QUADRANT = 32
GROUP = 16
BANKS = 8
LINE = 4
BIAS_ROW = P - 1
SCALE_ROW = P - BLOCKS
CHUNK = 128
CHUNKS = QUERIES // CHUNK
RAW_BYTES = 4 * PACK * CHUNK
SHARE = 48
PAIR = 2

FLOPS = 2 * FEATURES * LISTED * QUERIES
BYTES = 4 * FEATURES * QUERIES + (FEATURES + BLOCKS + 4) * NEURONS + 2 * P * LISTED // GROUP + 4 * LISTED * QUERIES


def tile_attend_neut_relu_topk_kernel(tc, qT, k_words, k_scales, nb, offs, out):
    nc = tc.nc
    with ExitStack() as ctx:
        keep = ctx.enter_context(tc.tile_pool(name="keep", bufs=1))
        shared = ctx.enter_context(tc.tile_pool(name="shared", bufs=1))
        psum = ctx.enter_context(tc.psum_pool(name="psum", bufs=1))

        def placed(shape, dtype, name, offset):
            return shared.tile(shape, dtype, name=name, align_bytes=64, offset=offset)

        raw_at = {1: 2 * RAW_BYTES, 2: 0, 3: RAW_BYTES}

        offsets = keep.tile([P, LISTED // GROUP], U16, name="offsets")

        def listed(table, first, count):
            return table.indirect(offsets[:, first * P // GROUP : (first + count) * P // GROUP])

        identity = keep.tile([P, P], F32, name="identity")
        nc.vector.memset(identity[:], 0.0)
        make_identity(nc, identity[:], nomemset=True)
        scale_table = placed([P, NEURONS], U8, "scale_table", RAW_BYTES // 2)
        nc.vector.memset(scale_table[0:SCALE_ROW, :].bitcast(I32), 0)
        k_scale = keep.tile([P, LISTED], U8, name="k_scale", align_bytes=64)
        nc.vector.memset(k_scale[:].bitcast(I32), 0)
        bias_table = keep.tile([P, NEURONS], F32, name="bias_table", align_bytes=64)
        nc.vector.memset(bias_table[0:BIAS_ROW, :].bitcast(I32), 0)
        word_table = keep.tile([P, NEURONS], I32, name="word_table", align_bytes=64)

        q_planes = qT[0].rearrange("(p t) q -> p t q", t=PACK)
        q_raw = [keep.tile([P, PACK, CHUNK], F32, name="q_raw0", align_bytes=64)]

        def load_chunk(c):
            if c > 0:
                q_raw.append(placed([P, PACK, CHUNK], F32, "q_raw%d" % c, raw_at[c]))
            nc.sync.dma_start(q_raw[c][:], q_planes[:, :, c * CHUNK : (c + 1) * CHUNK])

        nc.sync.dma_start(offsets[:], offs)
        nc.scalar.dma_start(scale_table[SCALE_ROW:P, :].bitcast(I32), k_scales[0].bitcast(I32))
        nc.scalar.dma_start(bias_table[BIAS_ROW:P, :], nb[BIAS_ROW:P, :])
        load_chunk(0)
        nc.sync.dma_start(word_table[:], k_words[0].rearrange("p n r -> p (n r)").bitcast(I32))
        load_chunk(1)

        scale_listed = keep.tile([P, LISTED], U8, name="scale_listed", align_bytes=64)
        nc.vector.tensor_copy(scale_listed[:], listed(scale_table[:], 0, TILES))
        for r in range(4):
            queue = (nc.sync, nc.scalar)[r % 2]
            queue.dma_start(k_scale[r:P:QUADRANT, :].bitcast(I32), scale_listed[SCALE_ROW + r : P : 4, :].bitcast(I32))
        load_chunk(2)
        load_chunk(3)

        grouped, q_codes = {}, {}
        q_scales = [keep.tile([P, CHUNK], U8, name="q_scales%d" % c, align_bytes=64) for c in range(CHUNKS)]

        def interleave(engine, c, first, last):
            dst = grouped[c][:, first:last, :].rearrange("p (c i) t -> p c t i", i=LINE)
            src = q_raw[c][:, :, first:last].rearrange("p t (c i) -> p c t i", i=LINE)
            if engine == "S":
                nc.scalar.activation(dst, src, COPY)
            elif engine == "G":
                nc.gpsimd.tensor_scalar(dst, src, 1.0, 0.0, MULT, ADD)
            else:
                nc.vector.tensor_copy(dst, src)

        def quantise(c):
            q_codes[c] = keep.tile([P, CHUNK], U32, name="q_codes%d" % c, align_bytes=64)
            nc.vector.quantize_mx(
                out=q_codes[c][:].bitcast(FP8X4),
                scales=q_scales[c][:],
                in_=grouped[c][:].rearrange("p c t -> p (c t)"),
            )

        grouped[0] = keep.tile([P, CHUNK, PACK], BF16, name="grouped0", align_bytes=64)
        interleave("S", 0, 0, CHUNK)

        bias, turned = [], []
        for pair in range(TILES // PAIR):
            bias_listed = keep.tile([P, PAIR * P], F32, name="bias_listed", tag="listed%d" % pair, align_bytes=64)
            if pair == 0:
                nc.vector.tensor_copy(bias_listed[:], listed(bias_table[:], PAIR * pair, PAIR))
            else:
                nc.scalar.activation(bias_listed[:], listed(bias_table[:], PAIR * pair, PAIR), COPY)
            turned.append(psum.tile([P, PAIR, P], F32, name="turned", tag="bank%d" % (BANKS - 2 + pair)))
            for n in range(PAIR):
                nc.tensor.transpose(turned[pair][:, n, :], bias_listed[:, n * P : (n + 1) * P], identity[:])
            bias.append(keep.tile([P, PAIR], F32, name="bias%d" % pair))

        def fetch_bias(pair):
            nc.scalar.copy(bias[pair][:], turned[pair][:, :, BIAS_ROW])

        fetch_bias(0)
        quantise(0)

        k_codes = []
        for first, count in ((0, PAIR), (PAIR, 1), (PAIR + 1, 1)):
            part = keep.tile([P, count * P], U32, name="k_codes%d" % first, align_bytes=64)
            nc.vector.tensor_copy(part[:], listed(word_table[:].bitcast(U32), first, count))
            k_codes.extend(part[:, n * P : (n + 1) * P] for n in range(count))

        out_tiles = out[0].rearrange("(j p) q -> p j q", p=P)

        def multiply(c, pair, readers, result, singly=False):
            columns = slice(c * CHUNK, (c + 1) * CHUNK)
            for n in range(PAIR):
                j = PAIR * pair + n
                acc = psum.tile([P, CHUNK], F32, name="acc", tag="bank%d" % ((TILES * c + j) % BANKS))
                nc.tensor.matmul_mx(
                    out=acc[:],
                    lhsT=k_codes[j].bitcast(FP8X4),
                    lhsT_scale=k_scale[:, j * P : (j + 1) * P],
                    rhs=q_codes[c][:].bitcast(FP8X4),
                    rhs_scale=q_scales[c][:],
                    start=True,
                    stop=True,
                )
                if readers[n] == "S":
                    nc.scalar.activation(result[:, n, :], acc[:], RELU, bias=bias[pair][:, n : n + 1])
                else:
                    nc.vector.tensor_scalar(result[:, n, :], acc[:], bias[pair][:, n : n + 1], 0.0, ADD, MAX)
                if singly:
                    nc.sync.dma_start(out_tiles[:, j, columns], result[:, n, :])
            if not singly:
                nc.sync.dma_start(out_tiles[:, PAIR * pair : PAIR * (pair + 1), columns], result)

        def result_tile(tag):
            return keep.tile([P, PAIR, CHUNK], F32, name="result", tag=tag, align_bytes=64)[:]

        grouped[1] = keep.tile([P, CHUNK, PACK], BF16, name="grouped1", tag="listed0", align_bytes=64)
        interleave("S", 1, 0, CHUNK - SHARE)
        interleave("G", 1, CHUNK - SHARE, CHUNK)
        fetch_bias(1)
        quantise(1)
        multiply(0, 0, "SS", result_tile("result00"), singly=True)
        grouped[2] = placed([P, CHUNK, PACK], BF16, "grouped2", raw_at[1] + RAW_BYTES // 2)
        interleave("V", 2, 0, CHUNK)
        multiply(0, 1, "VS", result_tile("listed0"))
        quantise(2)
        multiply(1, 0, "SS", result_tile("result10"))
        grouped[3] = placed([P, CHUNK, PACK], BF16, "grouped3", raw_at[2])
        interleave("V", 3, 0, CHUNK)
        multiply(1, 1, "VS", placed([P, PAIR, CHUNK], F32, "result11", raw_at[1] + RAW_BYTES // 2)[:])
        quantise(3)
        result2 = placed([P, TILES, CHUNK], F32, "result2", raw_at[3])
        for pair in range(TILES // PAIR):
            multiply(2, pair, "VS", result2[:, PAIR * pair : PAIR * (pair + 1), :])
        for pair in range(TILES // PAIR):
            multiply(3, pair, "VS", result_tile("result3%d" % pair))
